import numpy as np, ml_dtypes
CORES = [3,5,19,21,35,37,51,53,67,69]
N = 10
TOK, K, FT = 512, 3, 1
ROUTE = [[[0,4,9],[4,5,6],[1,6,8],[3,4,9],[3,5,7],[1,2,5],[2,7,8],[4,5,9],[2,4,8],[2,3,7],[1,4,5],[0,2,4],[2,3,4],[1,4,8],[3,7,8],[0,1,7],[0,3,8],[2,4,6],[2,5,6],[0,7,8],[2,6,9],[5,8,9],[2,5,6],[0,2,3],[1,6,7],[2,6,8],[2,4,7],[3,5,7],[0,4,9],[0,5,9],[0,6,9],[2,4,7],[5,6,9],[0,1,7],[2,4,5],[0,1,2],[0,1,7],[0,1,3],[2,3,5],[1,2,6],[1,2,3],[1,4,7],[3,6,8],[4,6,7],[6,7,9],[2,7,9],[7,8,9],[2,5,9],[2,3,8],[1,2,9],[0,1,4],[2,4,5],[3,7,8],[1,4,5],[1,3,5],[1,3,9],[4,5,8],[2,3,5],[2,3,6],[4,6,8],[2,5,7],[0,7,8],[1,2,3],[3,4,7],[1,3,7],[4,5,7],[4,8,9],[1,6,7],[0,2,5],[0,3,9],[1,2,4],[1,4,9],[1,7,8],[1,3,8],[4,6,7],[2,6,7],[2,6,9],[3,7,8],[4,6,9],[4,6,8],[1,4,7],[0,2,7],[0,4,6],[4,6,8],[0,2,6],[2,3,4],[0,1,2],[2,3,7],[0,1,3],[4,7,8],[1,6,8],[3,5,8],[1,8,9],[0,2,4],[3,6,9],[1,2,3],[5,7,8],[0,4,6],[0,2,9],[2,8,9],[0,6,8],[4,6,9],[0,3,6],[1,6,7],[2,3,7],[3,5,6],[1,2,8],[4,5,7],[1,8,9],[2,6,9],[1,3,5],[0,2,9],[0,6,9],[5,7,9],[0,2,3],[0,3,9],[6,8,9],[1,4,5],[0,1,9],[2,4,9],[0,2,3],[3,6,8],[0,1,2],[3,5,7],[1,4,7],[4,6,8],[0,2,6],[0,3,4],[2,3,9],[0,4,9],[4,8,9],[0,5,9],[0,3,7],[0,2,8],[3,7,9],[4,5,6],[3,7,9],[0,4,7],[1,7,9],[0,7,9],[0,1,7],[1,6,7],[2,8,9],[1,3,7],[0,5,6],[6,8,9],[1,2,6],[2,3,4],[2,7,9],[3,6,8],[1,5,9],[3,6,7],[3,7,9],[3,5,8],[0,2,8],[2,4,5],[4,7,9],[1,2,6],[1,2,9],[1,6,7],[2,3,8],[2,4,8],[1,4,6],[0,2,5],[1,4,6],[0,1,5],[3,4,8],[5,7,8],[0,2,6],[0,7,8],[1,3,4],[3,5,6],[1,4,8],[4,5,9],[1,4,6],[4,5,7],[4,7,9],[2,4,6],[0,3,6],[4,7,9],[0,7,9],[2,5,6],[0,1,7],[1,4,7],[4,8,9],[6,7,9],[0,1,2],[0,5,7],[0,1,8],[2,8,9],[1,3,6],[1,5,8],[0,1,2],[5,6,7],[4,5,8],[1,6,8],[3,6,8],[2,3,8],[0,1,3],[0,3,8],[0,5,8],[0,5,6],[0,1,5],[5,7,8],[3,4,9],[3,5,7],[6,7,9],[0,4,8],[3,7,8],[1,2,8],[0,4,8],[2,3,7],[0,1,4],[4,5,9],[1,5,6],[5,6,8],[0,3,8],[4,5,8],[2,6,9],[0,1,4],[0,7,8],[0,5,7],[0,1,7],[0,6,7],[0,6,9],[4,5,8],[1,2,9],[1,5,6],[3,4,9],[1,3,9],[0,1,7],[0,6,9],[2,3,7],[3,6,9],[1,3,4],[3,8,9],[4,5,6],[3,4,7],[4,5,9],[3,5,7],[4,6,8],[2,6,9],[1,3,9],[4,6,9],[1,3,5],[0,5,6],[0,2,8],[6,7,8],[2,6,7],[0,5,7],[1,4,5],[2,4,7],[1,5,8],[2,5,8],[1,2,3],[0,1,8],[2,6,9],[1,3,6],[1,4,9],[5,6,7],[1,2,3],[6,7,9],[2,3,5],[3,4,8],[1,5,8],[3,5,9],[0,2,5],[6,7,8],[1,3,7],[0,2,6],[4,8,9],[1,7,8],[2,3,5],[2,3,4],[1,4,8],[3,4,6],[2,5,9],[1,5,8],[0,7,9],[0,4,7],[4,5,9],[2,3,6],[1,7,8],[5,7,9],[1,4,9],[6,7,8],[2,5,7],[5,8,9],[3,6,8],[2,3,6],[1,2,3],[1,2,8],[3,7,8],[3,7,8],[1,3,6],[0,2,4],[2,4,5],[2,4,7],[0,1,9],[0,2,8],[2,4,6],[1,5,6],[0,1,5],[4,5,6],[2,6,9],[0,5,9],[2,5,8],[1,3,7],[0,3,9],[1,2,4],[2,3,8],[0,1,4],[1,7,9],[2,3,5],[1,2,3],[0,3,9],[2,3,7],[3,7,9],[0,1,3],[0,5,9],[3,7,9],[2,4,7],[2,6,7],[7,8,9],[2,5,9],[0,4,5],[5,6,9],[0,2,6],[2,7,9],[0,4,9],[0,4,6],[1,5,6],[0,3,5],[3,5,7],[3,4,9],[0,6,8],[5,6,8],[0,1,4],[0,2,3],[1,3,4],[3,4,6],[0,1,5],[1,2,8],[5,6,9],[4,7,9],[2,3,6],[1,2,4],[0,2,9],[0,8,9],[0,3,9],[3,5,8],[2,6,7],[0,2,8],[0,2,7],[2,4,5],[7,8,9],[6,7,8],[5,6,7],[4,5,6],[0,5,8],[0,1,3],[4,5,9],[2,3,4],[2,4,5],[0,2,6],[5,8,9],[2,4,6],[0,3,9],[6,7,9],[0,2,6],[0,1,4],[0,1,5],[2,4,5],[2,3,5],[0,2,4],[0,2,5],[0,2,4],[0,1,5],[1,6,8],[1,4,7],[1,6,9],[4,5,7],[1,6,9],[2,4,9],[0,3,7],[0,2,7],[5,8,9],[1,2,9],[2,4,7],[1,2,9],[3,4,8],[5,6,7],[4,7,8],[0,7,8],[3,5,7],[0,8,9],[0,3,9],[2,5,6],[0,1,5],[2,7,8],[2,4,5],[1,5,9],[3,5,7],[0,5,7],[3,5,6],[7,8,9],[1,4,5],[1,3,8],[1,5,8],[0,2,6],[5,8,9],[1,2,3],[0,3,9],[2,7,9],[1,4,6],[1,3,9],[0,8,9],[0,3,6],[1,2,8],[3,4,5],[0,5,9],[1,2,6],[1,6,8],[1,8,9],[3,4,9],[0,5,9],[1,5,9],[3,5,7],[4,5,7],[3,6,8],[4,6,9],[2,5,6],[1,3,8],[0,2,9],[1,2,9],[3,7,9],[0,7,9],[0,1,2],[2,3,8],[0,1,3],[4,6,8],[3,7,8],[1,3,7],[1,4,8],[5,6,7],[1,8,9],[2,6,9],[1,5,6],[3,8,9],[1,4,7],[3,6,7],[3,5,6],[2,4,9],[1,3,9],[3,6,7],[4,5,6],[5,8,9],[1,3,6],[1,5,6],[1,4,8],[2,4,6],[0,4,7],[1,4,8],[4,5,7],[1,6,9],[3,4,5],[5,6,9],[0,8,9],[0,4,7],[0,6,9],[4,5,9],[1,3,6],[1,2,3],[4,7,8],[0,2,7],[1,6,8],[1,3,7],[2,3,8],[7,8,9],[0,2,7],[0,2,6],[0,3,5],[1,7,9],[2,7,9],[0,3,7],[1,2,5],[2,4,7],[0,1,5],[3,7,9],[0,1,9],[2,6,7],[0,1,5],[4,5,6],[2,3,7],[4,8,9],[1,5,9],[0,5,7],[4,6,8],[0,6,8],[6,8,9],[2,3,4],[6,8,9],[2,7,8],[0,6,7],[1,7,8],[1,3,6],[0,3,4],[5,7,8],[0,1,4],[3,4,5],[3,6,9],[1,2,8]],[[0,4,5],[1,3,5],[4,5,7],[4,5,9],[5,7,9],[3,5,9],[1,7,8],[0,2,6],[1,3,8],[1,8,9],[2,6,8],[1,8,9],[0,6,9],[0,6,9],[1,4,5],[2,4,7],[0,3,6],[0,5,7],[1,4,8],[0,4,7],[2,6,7],[5,8,9],[0,4,5],[4,7,9],[1,2,5],[4,8,9],[2,3,4],[0,3,9],[4,5,9],[5,6,7],[3,4,5],[0,2,9],[0,5,6],[3,5,7],[0,1,8],[0,1,8],[0,2,3],[3,4,9],[6,8,9],[0,2,8],[6,7,8],[2,6,8],[1,6,8],[1,5,9],[1,2,4],[0,1,6],[3,8,9],[3,4,7],[0,1,5],[0,8,9],[4,6,8],[1,6,9],[1,5,7],[1,2,4],[1,4,9],[2,5,9],[3,7,8],[2,7,9],[1,2,7],[0,7,8],[4,7,8],[0,8,9],[0,3,9],[2,6,9],[3,5,9],[2,3,9],[2,5,6],[6,7,9],[2,4,5],[5,8,9],[1,3,8],[1,7,9],[5,6,9],[0,4,6],[6,7,8],[3,5,6],[3,6,9],[3,5,9],[5,7,9],[1,6,7],[0,2,9],[0,5,7],[3,5,9],[1,5,7],[0,2,5],[0,4,9],[2,4,8],[5,6,9],[0,5,9],[0,2,3],[2,3,5],[1,5,6],[0,3,7],[2,4,8],[2,6,7],[0,7,8],[2,3,6],[1,2,3],[1,2,8],[1,2,8],[2,7,9],[1,5,7],[1,4,6],[0,6,9],[1,7,8],[2,5,7],[0,2,3],[0,5,7],[2,3,4],[1,6,8],[3,5,6],[3,6,9],[6,7,9],[0,2,3],[0,2,4],[4,6,7],[1,7,9],[2,8,9],[0,5,8],[0,3,9],[1,4,8],[3,5,9],[0,3,4],[0,1,8],[0,3,5],[1,2,6],[3,5,8],[3,5,8],[1,5,7],[0,7,9],[0,3,8],[0,3,4],[4,7,8],[7,8,9],[5,6,7],[0,5,7],[2,7,9],[3,4,9],[2,6,9],[2,4,9],[4,6,7],[0,8,9],[1,7,8],[1,8,9],[2,4,9],[0,8,9],[2,4,8],[1,2,4],[1,5,9],[1,2,7],[0,1,6],[0,4,9],[2,4,7],[2,4,5],[3,6,8],[1,7,9],[4,6,9],[3,5,8],[0,1,6],[1,3,7],[0,6,9],[3,5,7],[3,4,8],[2,5,9],[0,3,4],[0,3,6],[3,5,7],[0,6,8],[1,7,8],[0,4,5],[4,5,6],[0,1,7],[4,7,9],[4,5,6],[6,7,9],[1,2,8],[0,1,7],[0,3,8],[1,3,7],[0,1,7],[4,6,8],[3,4,6],[1,2,5],[1,8,9],[0,1,6],[2,5,6],[0,6,9],[0,5,9],[0,1,4],[3,4,8],[4,7,8],[4,5,6],[3,5,7],[7,8,9],[3,5,8],[4,8,9],[0,2,7],[1,7,8],[0,1,9],[2,3,7],[1,4,5],[2,6,7],[7,8,9],[0,5,9],[0,7,8],[2,4,9],[4,5,7],[5,6,9],[6,7,8],[4,5,9],[3,4,8],[1,3,8],[1,3,6],[2,3,6],[1,5,9],[1,6,7],[1,3,5],[0,1,5],[2,3,9],[1,7,8],[0,2,5],[2,7,8],[0,1,4],[4,5,8],[2,5,9],[1,3,4],[3,4,6],[5,7,9],[0,1,6],[0,2,8],[2,4,9],[0,6,9],[2,6,8],[1,5,6],[1,6,8],[3,6,8],[5,7,8],[1,5,9],[0,2,8],[2,3,7],[2,4,9],[1,4,5],[1,3,7],[3,8,9],[4,6,8],[0,4,9],[1,3,9],[1,6,9],[5,6,8],[2,5,9],[2,6,8],[0,1,6],[5,7,9],[0,5,7],[2,7,9],[1,2,6],[0,1,6],[1,2,6],[1,3,7],[3,4,7],[2,5,6],[3,7,8],[5,7,8],[0,1,6],[3,4,5],[5,8,9],[2,5,9],[5,7,9],[1,6,8],[4,6,7],[0,3,6],[0,1,2],[1,4,6],[1,7,8],[5,6,8],[3,8,9],[0,5,6],[1,5,8],[0,3,4],[3,7,8],[2,4,5],[0,4,7],[5,6,9],[1,6,8],[1,3,4],[0,3,5],[0,5,6],[1,5,6],[1,4,9],[2,6,8],[2,3,4],[1,7,8],[2,5,8],[1,3,9],[2,5,9],[0,6,8],[0,1,6],[2,3,5],[0,5,6],[1,2,9],[0,4,6],[0,3,5],[0,2,5],[1,4,5],[2,5,9],[0,3,7],[5,7,9],[4,6,9],[2,3,7],[1,4,5],[3,8,9],[1,4,9],[2,5,7],[2,6,7],[0,2,7],[0,2,5],[0,4,9],[3,8,9],[4,6,7],[1,2,7],[3,5,6],[0,1,8],[0,6,8],[0,1,9],[1,5,7],[0,3,4],[0,3,8],[2,6,7],[4,8,9],[2,3,7],[0,1,4],[0,1,9],[2,8,9],[2,3,7],[5,7,8],[1,8,9],[0,1,7],[0,1,3],[0,4,8],[2,7,9],[0,4,7],[3,4,5],[0,1,3],[1,6,7],[3,4,9],[0,2,8],[0,1,6],[5,8,9],[3,6,9],[4,6,7],[0,3,8],[3,5,9],[2,6,9],[2,6,7],[0,3,8],[0,5,9],[4,7,9],[1,2,8],[2,3,4],[1,4,5],[4,7,9],[2,6,9],[2,5,7],[4,5,6],[2,3,4],[1,7,8],[0,1,2],[4,7,8],[3,8,9],[0,2,3],[0,1,6],[0,1,3],[0,5,9],[1,4,8],[3,4,6],[6,7,9],[3,7,9],[3,4,6],[0,4,8],[4,7,8],[1,4,5],[2,3,9],[0,1,9],[0,1,5],[0,4,9],[4,5,7],[0,4,9],[2,4,5],[5,8,9],[0,5,8],[3,5,8],[2,8,9],[2,3,8],[1,3,8],[3,4,8],[0,5,9],[0,3,6],[0,1,5],[0,2,8],[1,7,8],[0,8,9],[4,8,9],[0,5,8],[4,5,8],[1,2,7],[0,2,3],[0,1,9],[3,4,7],[0,2,8],[1,3,5],[3,4,7],[3,5,7],[0,2,8],[0,6,7],[2,3,7],[1,6,8],[0,3,6],[5,7,8],[2,4,5],[3,4,6],[1,5,9],[4,6,9],[0,5,8],[7,8,9],[0,3,4],[2,4,9],[3,7,8],[0,2,8],[5,6,9],[0,3,7],[3,6,8],[0,2,7],[1,2,3],[1,2,6],[4,5,6],[0,5,8],[3,5,7],[0,2,3],[1,5,9],[4,7,8],[0,1,8],[0,1,6],[0,3,7],[2,8,9],[3,5,9],[3,4,9],[0,2,4],[1,2,5],[0,1,7],[3,6,7],[0,1,5],[0,1,9],[0,1,3],[1,4,5],[1,6,9],[2,6,9],[0,2,8],[0,7,9],[0,6,9],[1,3,8],[1,4,7],[0,3,6],[0,6,7],[0,1,3],[3,8,9],[0,2,4],[1,5,6],[1,7,8],[4,5,6],[1,4,7],[0,2,5],[0,2,6],[0,8,9],[3,7,8],[2,3,9],[2,5,6],[1,3,6],[0,5,7],[0,6,9],[0,5,9],[2,5,8],[0,2,4],[0,6,8],[1,3,8],[4,6,9],[0,1,6],[0,5,8],[0,1,5],[0,1,8],[4,5,8],[5,7,9],[0,1,4],[3,4,8],[1,2,5],[1,6,8],[0,4,8],[0,2,5],[2,4,5],[7,8,9],[0,6,9],[1,4,7],[0,4,6],[0,6,8],[1,4,9],[4,5,8],[0,4,8],[0,4,9],[1,4,6],[2,4,6],[1,5,6],[1,3,7],[5,7,9]],[[0,2,6],[2,7,8],[0,2,3],[1,4,8],[1,3,8],[3,4,5],[0,7,9],[5,6,8],[0,7,9],[2,4,9],[4,7,8],[3,4,8],[0,2,8],[0,7,8],[3,6,8],[2,3,9],[2,6,9],[2,3,9],[0,3,9],[1,4,8],[1,3,7],[3,6,9],[2,3,5],[0,6,7],[0,2,8],[1,6,9],[0,2,8],[0,2,6],[3,4,7],[5,6,8],[0,7,9],[3,6,8],[1,5,6],[1,2,4],[1,7,9],[3,5,6],[0,1,3],[0,2,5],[1,2,9],[2,4,7],[0,5,7],[1,3,9],[4,5,9],[1,2,9],[2,3,4],[3,4,9],[2,3,9],[2,4,5],[0,4,7],[5,6,8],[0,4,6],[0,3,8],[2,5,7],[1,6,8],[4,6,7],[6,7,8],[3,5,7],[0,4,9],[3,6,9],[0,3,6],[0,3,8],[2,5,7],[1,5,7],[2,3,7],[4,8,9],[0,4,7],[1,2,5],[0,2,6],[2,7,8],[2,4,9],[0,2,6],[4,7,9],[1,5,8],[0,4,6],[1,3,4],[6,7,8],[1,4,8],[2,6,9],[1,6,7],[0,4,7],[0,5,7],[6,8,9],[1,8,9],[0,3,4],[2,4,5],[0,5,9],[1,2,5],[0,5,6],[0,2,8],[0,1,9],[2,6,9],[3,6,7],[0,2,7],[0,2,9],[1,7,9],[1,6,7],[4,8,9],[0,8,9],[1,6,8],[1,3,6],[2,7,9],[6,7,8],[2,4,6],[0,2,9],[3,7,9],[2,3,5],[2,4,6],[1,2,9],[4,5,8],[0,1,6],[2,3,5],[0,3,4],[2,8,9],[0,1,9],[0,6,7],[0,1,6],[2,4,8],[3,4,7],[1,4,7],[0,4,8],[1,3,8],[0,8,9],[3,7,8],[0,1,3],[0,2,6],[1,7,9],[0,7,9],[1,5,8],[0,1,7],[1,4,7],[2,5,8],[3,7,9],[4,6,9],[2,3,7],[2,3,9],[1,4,7],[2,4,6],[2,4,7],[1,6,9],[1,5,7],[1,5,9],[0,6,9],[0,2,9],[6,8,9],[5,6,8],[1,6,8],[7,8,9],[1,2,6],[2,8,9],[5,8,9],[1,3,5],[0,3,4],[1,8,9],[0,4,8],[3,5,6],[1,2,4],[6,8,9],[5,7,8],[1,2,5],[0,4,5],[2,7,8],[0,2,8],[1,4,5],[2,6,7],[5,7,9],[1,3,5],[0,1,7],[2,4,8],[5,7,8],[1,2,6],[0,2,7],[0,3,5],[0,7,8],[3,4,6],[0,5,6],[4,8,9],[1,7,9],[0,1,7],[6,7,9],[2,6,8],[1,8,9],[4,5,9],[2,5,9],[2,3,4],[1,7,9],[0,3,4],[0,7,9],[0,5,9],[0,5,6],[3,5,9],[2,4,7],[1,4,7],[1,2,3],[2,3,6],[1,8,9],[4,5,6],[1,6,9],[1,4,6],[0,4,5],[1,5,8],[4,7,9],[2,4,7],[0,2,7],[1,3,4],[4,8,9],[3,8,9],[0,4,7],[0,1,4],[5,6,9],[2,7,8],[4,8,9],[2,3,6],[0,2,6],[2,5,7],[4,5,6],[0,1,4],[0,2,4],[4,5,6],[0,1,7],[1,8,9],[1,2,3],[2,4,6],[4,6,7],[2,3,9],[2,7,8],[7,8,9],[0,5,9],[0,3,9],[1,4,5],[2,3,6],[4,5,7],[1,5,9],[1,2,4],[0,1,3],[0,3,9],[0,1,2],[0,2,8],[1,4,6],[0,5,9],[3,4,6],[6,7,8],[1,5,8],[0,1,2],[5,6,7],[4,6,7],[3,5,8],[0,4,7],[1,3,6],[2,4,9],[1,3,9],[1,4,9],[0,2,3],[3,6,9],[0,1,2],[3,7,9],[1,6,7],[1,3,5],[1,3,9],[0,6,7],[1,3,6],[0,3,8],[3,7,8],[0,1,2],[3,4,6],[3,5,9],[1,7,9],[3,7,9],[0,1,5],[1,4,7],[0,2,3],[1,6,7],[1,4,7],[0,1,2],[2,7,9],[1,2,5],[1,5,7],[0,2,4],[5,6,9],[1,2,9],[3,4,8],[2,5,8],[1,2,8],[0,2,4],[0,2,3],[1,3,8],[1,2,9],[2,6,7],[1,6,7],[3,7,9],[1,6,8],[0,1,8],[1,5,9],[1,4,7],[0,2,8],[4,7,8],[0,4,6],[1,2,4],[2,5,7],[0,1,5],[0,5,8],[2,5,9],[3,4,8],[1,7,8],[1,4,9],[0,2,6],[0,4,7],[1,2,8],[2,4,6],[3,6,8],[3,4,6],[1,5,6],[2,6,9],[1,6,7],[0,3,4],[2,6,9],[0,6,7],[4,6,7],[0,2,7],[3,5,9],[5,6,8],[1,6,7],[0,3,9],[2,3,9],[2,4,7],[2,3,4],[1,4,8],[3,5,9],[6,7,9],[0,5,6],[0,4,8],[0,2,9],[0,6,7],[3,7,8],[2,4,6],[0,1,7],[3,4,9],[0,2,5],[2,4,9],[0,6,9],[4,8,9],[0,1,2],[3,7,9],[2,3,7],[2,4,7],[4,7,8],[2,5,8],[0,2,4],[2,7,8],[1,2,4],[6,7,8],[7,8,9],[2,4,7],[1,3,5],[1,7,9],[0,6,7],[0,3,4],[2,6,8],[2,5,7],[0,1,8],[3,7,8],[3,4,7],[6,7,9],[5,7,9],[1,6,9],[0,6,9],[6,8,9],[4,8,9],[0,4,8],[5,8,9],[2,3,4],[0,2,8],[0,2,6],[2,4,7],[1,4,7],[0,7,8],[3,8,9],[0,6,9],[2,3,9],[4,7,9],[0,4,6],[0,2,3],[1,3,7],[2,3,7],[4,6,7],[2,7,9],[0,3,6],[0,1,5],[4,5,6],[3,4,5],[5,7,8],[0,2,6],[3,4,8],[0,7,9],[3,4,7],[4,7,8],[1,2,8],[6,7,9],[0,1,4],[2,4,8],[0,2,3],[0,4,6],[1,3,7],[0,2,5],[3,4,8],[4,7,8],[1,3,6],[1,8,9],[0,1,5],[0,1,4],[1,2,5],[1,5,9],[1,2,9],[0,4,9],[3,6,8],[0,2,3],[1,6,7],[4,5,9],[1,3,9],[5,7,8],[3,4,6],[1,3,9],[0,1,6],[2,7,9],[1,5,8],[4,5,7],[1,3,9],[0,7,8],[2,5,6],[2,7,8],[2,4,6],[1,3,9],[1,6,7],[4,6,8],[1,3,8],[0,1,4],[1,4,9],[1,7,8],[1,3,9],[0,6,9],[3,6,7],[0,7,8],[2,8,9],[0,2,4],[4,5,9],[1,3,8],[4,5,6],[5,7,8],[4,5,9],[2,7,9],[1,4,9],[7,8,9],[1,6,7],[4,8,9],[3,4,9],[0,7,8],[0,4,6],[1,4,8],[3,4,9],[1,6,8],[3,6,7],[3,5,8],[0,4,5],[0,3,4],[2,6,8],[1,2,3],[0,1,3],[5,7,8],[6,7,8],[1,4,5],[1,6,8],[1,2,7],[0,2,4],[3,5,9],[0,3,4],[1,3,8],[3,6,8],[0,5,6],[1,5,8],[2,3,9],[2,6,8],[5,7,8],[5,7,9],[0,3,8],[0,1,9],[0,1,9],[5,6,7],[1,5,7],[1,6,9],[3,6,8],[1,3,9],[2,3,9],[0,3,9],[1,7,9],[3,4,8],[0,3,4],[0,1,8],[6,8,9],[1,3,8],[2,8,9],[3,4,7],[0,1,8],[1,3,4],[1,3,7],[1,4,8],[1,4,6],[0,7,9],[1,4,5],[1,2,3],[2,5,6],[0,2,7],[2,5,6],[3,4,6]],[[1,3,8],[1,3,9],[6,7,8],[1,2,8],[3,6,9],[3,5,9],[2,3,4],[2,5,9],[0,3,8],[5,8,9],[1,6,7],[0,2,6],[3,6,9],[2,4,7],[2,3,8],[0,7,8],[0,4,6],[3,6,7],[2,5,9],[3,7,8],[3,4,7],[0,2,9],[1,3,4],[2,7,8],[0,4,8],[0,7,9],[1,3,8],[2,4,6],[5,6,7],[3,4,7],[0,3,7],[1,4,7],[3,6,8],[2,5,9],[2,5,8],[0,4,8],[0,2,3],[4,6,7],[2,6,8],[0,8,9],[2,3,8],[4,5,8],[1,3,4],[5,6,7],[0,4,9],[5,6,7],[3,6,8],[2,4,7],[0,7,9],[2,3,5],[1,2,7],[2,5,8],[1,3,5],[0,1,9],[2,3,5],[4,5,6],[2,4,5],[0,2,8],[4,5,7],[1,4,6],[0,6,9],[3,7,8],[4,6,8],[1,5,7],[3,4,5],[2,4,7],[4,7,9],[4,8,9],[0,4,8],[3,4,7],[0,7,9],[3,5,6],[0,5,8],[0,1,6],[1,5,9],[1,3,7],[4,7,8],[0,1,8],[3,6,8],[0,2,7],[1,3,6],[0,2,4],[2,5,9],[2,3,5],[2,5,9],[3,5,8],[2,6,9],[0,1,4],[0,3,9],[2,6,9],[1,7,8],[3,4,5],[3,4,6],[1,3,5],[2,7,9],[1,5,8],[2,6,8],[4,7,9],[0,1,6],[0,5,9],[4,6,8],[2,5,7],[1,4,8],[0,1,7],[2,5,8],[2,4,9],[1,2,5],[6,8,9],[1,2,3],[0,5,6],[4,5,9],[3,4,5],[3,4,6],[6,8,9],[2,5,7],[0,6,7],[3,6,9],[0,6,7],[0,3,8],[2,6,7],[6,7,9],[1,3,9],[6,7,8],[4,7,9],[7,8,9],[0,5,8],[1,4,6],[1,4,5],[2,7,8],[2,4,9],[2,7,8],[2,3,9],[1,5,8],[2,4,5],[3,7,8],[3,8,9],[0,3,4],[0,3,4],[2,6,9],[2,5,7],[1,6,8],[1,3,6],[3,5,9],[0,2,6],[1,5,7],[2,6,8],[2,7,8],[0,5,6],[1,3,5],[3,6,7],[0,4,7],[3,4,9],[1,2,5],[2,4,7],[2,7,8],[1,2,9],[2,4,8],[0,5,8],[0,1,4],[1,6,8],[0,2,9],[2,4,6],[2,3,9],[2,3,9],[5,6,9],[2,7,9],[1,4,5],[3,4,5],[1,3,6],[0,3,4],[1,4,9],[4,6,8],[0,2,3],[2,8,9],[2,5,7],[7,8,9],[0,3,9],[0,5,6],[4,7,9],[0,3,9],[0,3,6],[0,1,8],[1,3,9],[2,4,5],[0,5,7],[0,1,8],[5,6,7],[1,4,8],[2,7,9],[0,8,9],[2,7,9],[5,8,9],[0,3,4],[3,5,7],[5,6,8],[2,5,7],[5,6,7],[1,4,8],[1,3,5],[1,5,6],[2,6,7],[2,4,8],[5,8,9],[2,3,8],[2,6,8],[2,8,9],[3,7,8],[0,5,6],[0,2,9],[1,4,6],[2,4,7],[1,8,9],[0,1,9],[4,6,7],[3,4,5],[0,4,9],[0,4,9],[2,6,7],[1,2,9],[2,8,9],[3,5,7],[1,6,7],[0,5,7],[4,6,9],[3,4,6],[0,1,4],[0,7,9],[3,4,5],[3,7,9],[1,2,4],[2,3,7],[1,5,7],[2,4,5],[1,6,8],[3,8,9],[0,1,6],[0,3,7],[2,4,9],[4,5,9],[3,4,7],[2,8,9],[1,7,9],[1,5,8],[7,8,9],[2,4,7],[2,3,5],[1,7,8],[4,5,9],[5,6,9],[0,5,7],[4,5,9],[0,5,9],[1,5,7],[0,5,7],[1,2,3],[7,8,9],[1,3,5],[0,5,7],[2,3,5],[0,1,2],[0,4,8],[0,2,7],[0,7,8],[1,2,4],[1,5,7],[2,4,6],[0,2,3],[1,3,6],[0,5,6],[1,3,6],[1,3,5],[0,1,4],[0,1,4],[0,4,6],[3,6,8],[2,4,8],[2,4,6],[2,4,7],[0,7,8],[2,5,6],[2,5,7],[0,4,6],[1,3,8],[3,6,8],[1,3,5],[4,7,8],[3,5,9],[0,7,8],[3,6,8],[4,6,7],[0,3,5],[0,2,8],[2,3,7],[4,6,7],[3,4,8],[0,7,8],[0,4,5],[0,1,9],[6,7,9],[1,3,6],[0,3,4],[2,6,9],[2,3,4],[5,6,9],[0,1,8],[2,8,9],[1,2,5],[4,6,8],[4,6,8],[2,3,4],[1,7,8],[0,1,5],[1,2,5],[2,3,5],[3,6,9],[1,2,8],[1,4,8],[3,6,7],[3,5,8],[0,3,6],[2,3,7],[0,2,3],[0,1,8],[4,6,8],[5,6,9],[0,1,3],[0,4,8],[2,4,7],[3,8,9],[1,2,8],[0,1,6],[1,2,9],[0,8,9],[3,6,9],[0,1,8],[1,3,4],[0,1,9],[6,7,8],[2,4,5],[1,4,5],[1,3,4],[1,6,8],[1,3,4],[3,7,9],[1,3,6],[1,4,7],[1,3,9],[0,5,8],[4,6,9],[0,1,9],[1,4,8],[0,2,3],[2,7,8],[2,6,7],[0,2,4],[1,4,5],[0,2,5],[3,4,6],[0,4,8],[3,4,6],[1,7,9],[1,3,5],[0,2,3],[5,8,9],[0,4,9],[0,6,8],[0,3,5],[1,7,9],[7,8,9],[1,3,4],[0,5,9],[2,3,7],[2,3,6],[1,2,5],[3,4,8],[1,5,9],[1,3,5],[1,4,6],[0,2,3],[5,8,9],[0,5,8],[1,5,9],[1,7,9],[1,7,8],[2,3,7],[1,2,4],[2,4,6],[1,4,9],[2,3,7],[2,6,7],[4,5,8],[1,2,4],[3,7,9],[0,3,8],[0,3,8],[4,6,7],[3,4,7],[3,4,5],[0,3,6],[1,4,8],[0,2,9],[2,4,7],[2,3,4],[2,5,6],[3,4,8],[0,5,7],[1,2,4],[2,8,9],[1,3,6],[1,4,6],[0,5,7],[3,7,9],[4,6,9],[0,6,7],[4,7,9],[0,1,6],[0,3,5],[0,5,7],[1,3,8],[0,6,7],[3,8,9],[1,2,5],[5,7,8],[1,2,3],[4,7,8],[2,3,5],[0,7,8],[2,3,8],[0,3,9],[1,6,8],[0,4,7],[0,2,3],[5,7,9],[3,4,8],[1,3,9],[1,7,9],[2,3,9],[3,6,9],[4,5,6],[4,7,9],[1,7,9],[2,8,9],[3,4,7],[2,3,4],[0,2,9],[0,6,9],[3,8,9],[1,4,8],[4,5,7],[2,3,5],[1,3,5],[0,2,7],[6,8,9],[3,4,7],[2,4,7],[0,1,8],[0,1,7],[3,5,7],[0,5,8],[1,3,5],[0,6,7],[0,2,8],[3,5,9],[4,6,7],[1,4,6],[3,4,6],[0,3,5],[5,7,9],[0,6,9],[0,1,8],[1,4,7],[4,6,7],[2,5,6],[0,3,6],[3,4,6],[0,2,5],[0,3,7],[0,3,6],[2,4,8],[0,3,6],[0,6,8],[3,7,8],[1,2,5],[0,2,4],[2,4,5],[0,2,8],[1,3,4],[1,8,9],[3,5,7],[0,3,8],[2,5,7],[3,6,9],[3,4,5],[2,3,4],[1,2,7],[0,1,2],[3,6,9],[2,3,5],[1,3,5],[3,5,8],[3,6,8],[3,5,7],[3,5,8],[5,8,9],[1,7,8],[4,5,7],[0,7,9],[1,4,5],[0,1,4],[0,3,6],[0,3,9],[0,5,6]],[[1,3,5],[4,7,8],[0,7,9],[2,8,9],[1,2,4],[1,4,8],[0,2,9],[0,3,5],[1,5,6],[5,8,9],[1,6,9],[6,7,9],[4,6,8],[3,4,6],[3,5,9],[6,7,8],[0,2,9],[0,4,7],[0,4,5],[3,8,9],[7,8,9],[0,2,8],[2,7,9],[2,5,9],[6,8,9],[0,2,5],[0,3,5],[1,5,7],[1,2,9],[5,6,7],[1,2,9],[0,4,6],[1,4,6],[0,1,5],[3,6,8],[1,4,7],[0,6,8],[2,5,8],[0,2,8],[1,6,8],[0,8,9],[1,4,7],[0,1,6],[6,7,8],[3,4,5],[5,8,9],[2,3,4],[2,3,5],[0,1,8],[2,5,8],[0,3,8],[1,4,9],[2,3,9],[1,2,3],[0,3,7],[0,4,6],[2,5,9],[1,5,6],[0,6,8],[3,7,8],[4,5,6],[4,6,8],[3,4,7],[5,6,9],[1,3,6],[1,3,9],[0,1,2],[5,8,9],[4,7,8],[1,8,9],[0,6,8],[6,7,8],[1,2,4],[2,3,7],[0,1,5],[0,1,2],[1,5,9],[5,7,8],[0,2,5],[7,8,9],[4,6,9],[5,6,8],[4,6,9],[4,7,9],[1,2,4],[1,2,5],[5,7,8],[0,1,5],[0,2,4],[3,4,6],[3,6,9],[0,5,8],[5,6,9],[3,6,8],[0,5,8],[0,3,5],[1,2,4],[0,6,8],[0,3,4],[1,2,8],[1,3,9],[0,6,9],[3,6,9],[2,4,6],[5,6,9],[0,2,6],[2,3,8],[5,6,9],[2,3,9],[2,4,7],[0,7,8],[0,1,2],[1,3,5],[1,2,7],[0,3,4],[4,8,9],[6,7,9],[0,2,4],[4,5,9],[1,3,8],[3,7,9],[3,4,9],[4,5,8],[0,2,4],[0,2,6],[3,8,9],[0,1,7],[0,4,8],[1,7,8],[0,4,6],[1,3,9],[2,6,8],[0,3,4],[3,4,6],[0,6,9],[5,6,9],[0,3,7],[2,4,9],[0,2,3],[4,6,9],[0,2,4],[2,3,9],[1,3,4],[2,5,6],[0,4,7],[1,6,9],[6,7,9],[2,7,8],[1,2,7],[4,5,8],[1,4,7],[1,3,8],[1,2,9],[0,3,9],[1,2,5],[4,8,9],[0,2,5],[0,3,4],[1,4,7],[3,5,7],[4,8,9],[1,7,8],[5,7,9],[1,5,7],[3,4,6],[0,7,8],[1,7,9],[1,3,8],[2,7,9],[4,7,8],[2,5,9],[0,4,5],[2,5,7],[0,3,6],[2,6,8],[6,8,9],[6,8,9],[2,5,7],[0,3,9],[4,6,8],[3,5,7],[6,7,9],[1,2,7],[0,5,6],[4,5,8],[2,4,9],[0,3,9],[1,3,5],[3,6,8],[0,6,9],[1,2,9],[0,1,5],[1,6,8],[1,2,8],[1,8,9],[0,4,6],[3,7,8],[0,1,7],[2,3,4],[3,5,9],[2,5,8],[0,2,8],[0,5,9],[0,6,8],[0,2,4],[1,8,9],[6,7,8],[1,7,9],[2,3,7],[0,5,9],[2,3,4],[0,1,2],[3,4,9],[0,1,9],[1,5,8],[3,4,6],[1,2,6],[2,5,9],[4,5,6],[5,7,9],[0,3,7],[5,7,8],[1,2,4],[0,3,9],[0,1,4],[2,3,5],[0,6,9],[2,3,6],[3,6,7],[1,8,9],[0,5,7],[2,4,7],[1,4,9],[0,6,7],[1,4,7],[2,5,7],[3,5,8],[4,5,6],[2,7,9],[1,3,5],[2,3,6],[0,3,6],[1,2,7],[1,3,5],[2,3,8],[1,4,9],[0,5,9],[2,7,9],[2,4,6],[1,3,5],[3,7,9],[1,5,9],[3,5,7],[4,5,9],[2,3,5],[2,3,9],[0,1,7],[3,5,7],[2,5,8],[2,7,8],[5,6,9],[4,5,9],[2,5,7],[3,4,5],[1,2,6],[0,4,9],[0,6,7],[1,4,9],[0,3,5],[0,2,7],[5,6,9],[3,7,8],[5,6,9],[1,6,9],[2,4,8],[0,3,6],[1,5,7],[5,6,7],[3,5,6],[0,5,6],[4,5,9],[5,8,9],[1,4,6],[0,1,6],[1,6,8],[4,8,9],[1,4,6],[0,4,7],[2,4,6],[0,5,6],[1,2,5],[4,6,8],[0,5,9],[1,2,5],[1,2,7],[0,1,6],[2,3,8],[2,4,8],[1,2,7],[4,8,9],[6,7,8],[1,6,8],[0,2,7],[0,3,5],[3,4,5],[3,6,8],[0,5,7],[0,1,6],[0,3,9],[2,5,8],[2,4,9],[0,6,8],[0,2,4],[0,2,5],[0,2,4],[2,8,9],[0,1,5],[0,2,6],[3,4,9],[0,8,9],[1,4,8],[1,3,9],[0,4,7],[0,3,5],[4,5,9],[0,3,4],[3,7,9],[2,3,8],[1,4,6],[2,6,8],[2,3,4],[2,7,9],[5,6,7],[2,4,6],[3,6,9],[5,7,8],[1,5,6],[0,1,5],[1,3,9],[3,6,9],[1,4,9],[2,4,6],[1,6,7],[2,4,5],[1,2,6],[5,7,9],[1,5,8],[1,6,7],[1,2,6],[0,2,6],[0,2,8],[1,7,8],[1,5,6],[3,5,8],[0,3,5],[3,4,7],[0,5,7],[1,5,9],[1,2,7],[0,4,8],[5,6,8],[0,2,6],[1,2,3],[2,6,7],[4,5,6],[2,4,5],[0,2,6],[2,3,5],[0,3,5],[2,7,9],[2,5,6],[1,2,6],[3,4,9],[0,3,4],[2,3,9],[0,6,9],[0,1,6],[2,8,9],[3,7,9],[1,3,8],[4,7,8],[6,7,8],[4,5,8],[1,4,7],[0,3,5],[0,5,6],[0,3,7],[0,3,5],[0,1,8],[6,7,9],[2,5,6],[0,4,6],[0,2,4],[2,4,7],[2,6,8],[1,2,8],[1,6,8],[1,4,7],[2,4,6],[1,3,6],[3,6,8],[1,4,7],[1,4,7],[2,3,6],[1,6,9],[1,6,9],[4,8,9],[0,1,7],[1,3,4],[1,2,8],[1,4,5],[1,2,4],[2,8,9],[1,4,8],[1,6,7],[2,3,4],[1,5,9],[0,2,8],[5,6,9],[2,3,9],[1,2,7],[1,3,4],[5,7,8],[3,5,8],[2,3,7],[6,8,9],[4,5,7],[3,8,9],[3,8,9],[5,8,9],[2,7,8],[4,7,9],[6,8,9],[1,2,8],[0,1,4],[4,7,9],[1,2,3],[1,6,9],[0,1,3],[1,2,9],[6,8,9],[3,5,8],[0,1,2],[5,6,7],[0,4,8],[2,5,6],[0,2,5],[1,5,9],[0,5,7],[5,8,9],[1,3,7],[0,5,6],[7,8,9],[2,5,9],[0,4,7],[3,5,9],[0,3,6],[1,2,8],[0,5,6],[4,8,9],[0,6,9],[2,5,9],[0,5,9],[1,4,8],[0,1,2],[1,3,9],[1,2,7],[1,2,8],[0,4,5],[5,8,9],[0,5,6],[3,5,6],[0,2,8],[1,4,6],[0,3,7],[0,4,6],[7,8,9],[2,4,6],[1,8,9],[0,5,9],[2,4,6],[0,4,5],[2,5,8],[0,1,3],[3,6,9],[0,2,9],[2,3,7],[0,6,7],[3,6,9],[2,3,7],[1,3,5],[2,8,9],[3,6,8],[4,8,9],[4,5,7],[2,4,7],[1,2,7],[5,8,9],[2,3,6],[0,5,7],[0,4,5],[2,5,8],[0,3,4],[3,8,9],[1,2,8],[2,3,9],[5,7,9],[0,2,9],[0,4,5],[1,3,9],[2,7,8],[1,3,4]],[[2,3,4],[2,3,4],[0,4,9],[1,3,7],[0,2,6],[4,7,8],[1,5,9],[6,7,8],[0,2,8],[3,5,9],[0,3,6],[0,2,7],[1,2,6],[3,5,8],[3,4,6],[1,5,9],[0,1,2],[1,3,6],[2,3,7],[1,2,4],[4,8,9],[1,5,8],[1,2,7],[0,1,3],[0,3,7],[3,5,7],[1,4,5],[0,5,6],[0,3,8],[2,3,5],[4,5,9],[2,3,5],[3,4,5],[0,3,5],[1,2,6],[2,4,6],[2,6,9],[1,3,4],[4,5,8],[3,6,8],[1,2,9],[1,2,6],[1,2,9],[0,1,4],[0,6,8],[1,3,4],[1,3,4],[1,3,9],[3,5,9],[1,2,9],[0,6,8],[5,6,7],[2,4,7],[3,4,8],[3,7,9],[0,2,9],[2,5,6],[1,2,4],[3,4,8],[3,4,9],[5,6,9],[2,6,7],[4,7,8],[5,6,8],[0,7,8],[4,5,7],[1,5,7],[2,3,8],[4,6,9],[1,6,9],[0,4,5],[3,5,9],[4,5,9],[4,7,9],[0,1,7],[6,7,8],[2,3,4],[1,7,8],[3,5,7],[3,5,7],[2,5,8],[4,5,7],[0,1,3],[1,2,5],[0,1,7],[0,2,7],[1,6,8],[6,8,9],[0,1,7],[6,8,9],[1,3,6],[1,5,9],[3,5,9],[6,8,9],[0,4,7],[1,6,9],[0,1,5],[2,5,9],[3,5,6],[5,6,8],[0,5,7],[5,8,9],[4,5,8],[3,6,9],[2,4,8],[2,5,8],[0,2,5],[2,3,4],[1,2,9],[0,8,9],[1,4,5],[0,1,5],[0,1,4],[0,6,8],[7,8,9],[1,6,8],[3,5,6],[4,7,9],[1,5,8],[2,3,7],[1,5,7],[0,1,4],[4,8,9],[1,2,9],[1,2,9],[2,3,6],[1,5,6],[5,8,9],[1,2,5],[2,5,8],[0,2,7],[0,4,7],[4,8,9],[3,4,8],[3,5,9],[0,3,5],[0,5,7],[4,6,9],[7,8,9],[2,3,6],[2,7,9],[0,5,7],[1,2,3],[1,8,9],[3,6,8],[1,2,3],[0,3,6],[1,3,9],[2,3,8],[0,4,5],[5,6,7],[3,4,7],[3,5,9],[2,4,9],[1,4,6],[0,2,8],[3,6,8],[2,3,7],[1,2,3],[0,2,8],[0,1,6],[1,2,3],[1,6,9],[0,2,9],[1,4,8],[2,4,8],[2,3,7],[0,2,4],[0,1,3],[2,3,5],[0,1,2],[3,5,7],[3,6,8],[1,4,8],[3,7,9],[1,4,7],[2,6,7],[0,6,7],[6,8,9],[0,2,6],[3,4,7],[2,3,7],[7,8,9],[1,5,7],[3,7,8],[4,7,8],[1,2,7],[1,5,9],[3,7,8],[4,5,6],[0,1,6],[1,5,6],[0,5,6],[1,4,7],[2,3,4],[2,8,9],[2,4,8],[2,4,5],[2,6,8],[0,8,9],[2,7,8],[3,5,7],[6,7,9],[3,4,9],[1,3,6],[3,7,9],[1,5,9],[2,3,6],[4,6,9],[0,7,8],[3,5,9],[0,1,6],[2,3,9],[1,3,9],[2,7,8],[5,6,9],[1,4,9],[0,6,7],[1,6,8],[4,8,9],[0,1,7],[0,5,8],[3,4,5],[3,5,7],[0,2,3],[3,5,8],[3,6,9],[0,4,5],[1,4,9],[0,2,3],[4,8,9],[2,7,8],[0,5,9],[5,8,9],[0,3,8],[1,6,9],[2,4,5],[0,3,5],[0,2,8],[2,5,7],[3,7,9],[0,1,6],[4,6,8],[5,6,9],[3,4,6],[2,5,6],[2,3,8],[5,6,7],[1,3,9],[4,6,8],[2,4,8],[2,3,7],[2,4,7],[2,3,4],[0,5,7],[3,5,8],[0,3,7],[4,6,9],[0,7,8],[2,4,8],[4,8,9],[2,4,9],[2,7,8],[4,6,8],[4,8,9],[1,3,8],[5,6,7],[3,5,9],[0,6,7],[5,6,8],[1,3,6],[1,8,9],[3,4,9],[1,8,9],[1,2,7],[2,5,8],[1,4,9],[0,4,5],[2,6,9],[5,6,8],[0,2,5],[1,4,9],[0,4,7],[4,6,8],[2,6,7],[0,2,4],[3,6,9],[2,4,6],[1,2,9],[1,2,4],[1,5,6],[0,6,9],[3,7,9],[6,7,9],[1,3,6],[2,4,7],[2,3,6],[2,6,9],[1,2,6],[0,4,5],[0,6,7],[3,5,7],[1,5,9],[1,6,7],[0,6,7],[0,2,6],[1,6,7],[3,4,6],[3,5,9],[2,4,7],[0,1,6],[4,6,9],[1,7,9],[4,6,8],[1,2,5],[0,1,8],[3,7,9],[1,7,8],[1,6,9],[1,8,9],[0,3,9],[1,3,4],[3,5,8],[2,8,9],[0,3,5],[0,2,6],[2,5,6],[1,2,6],[2,3,7],[0,8,9],[0,2,4],[0,3,6],[2,3,6],[0,4,9],[0,6,8],[3,7,8],[0,1,7],[1,6,7],[0,3,9],[1,4,7],[3,4,6],[1,5,8],[0,1,8],[4,7,8],[2,3,6],[2,3,9],[1,2,4],[0,3,5],[0,5,8],[5,6,7],[2,6,7],[4,8,9],[0,7,8],[0,3,9],[2,4,9],[1,4,8],[0,3,5],[1,2,7],[5,6,8],[1,4,6],[4,6,9],[1,3,7],[2,3,5],[0,4,5],[0,3,7],[1,6,9],[0,5,6],[0,3,9],[4,7,8],[0,1,9],[1,3,8],[5,8,9],[7,8,9],[0,4,8],[0,1,8],[0,2,8],[1,4,8],[3,4,5],[2,5,8],[0,7,9],[2,3,8],[3,6,8],[4,7,8],[3,5,9],[5,8,9],[0,3,9],[0,2,5],[1,2,8],[0,7,8],[3,5,7],[0,2,3],[0,3,4],[2,3,6],[0,8,9],[7,8,9],[1,5,9],[2,3,5],[0,3,9],[4,5,6],[1,3,9],[4,5,9],[0,3,5],[3,7,8],[3,7,9],[0,3,7],[1,3,9],[0,1,3],[1,4,8],[4,5,7],[0,3,8],[0,5,8],[3,5,6],[3,6,7],[0,2,6],[3,4,8],[0,6,7],[0,3,8],[5,8,9],[1,3,8],[4,7,9],[3,5,6],[3,6,8],[3,6,9],[0,5,6],[1,7,8],[6,7,8],[1,3,7],[0,2,5],[6,7,8],[2,3,9],[6,7,8],[0,1,8],[0,4,8],[1,4,5],[3,4,8],[0,6,9],[0,3,9],[5,6,9],[4,6,7],[2,4,8],[1,3,6],[3,6,8],[3,6,8],[2,3,9],[1,4,9],[2,4,8],[2,7,8],[2,4,7],[2,8,9],[0,6,7],[0,4,8],[0,3,4],[1,5,6],[4,6,8],[0,8,9],[1,6,8],[0,3,4],[1,5,6],[1,4,7],[0,2,5],[4,5,9],[2,3,8],[2,5,8],[1,4,9],[1,2,3],[1,4,5],[0,5,8],[4,6,9],[1,2,8],[1,3,6],[0,2,6],[1,3,6],[2,7,8],[5,7,9],[3,5,8],[3,6,9],[1,6,8],[1,2,6],[2,3,4],[1,6,8],[0,7,9],[0,6,8],[0,4,6],[0,1,5],[2,3,8],[1,3,4],[0,8,9],[7,8,9],[6,7,9],[5,6,9],[4,7,9],[0,5,9],[1,3,5],[2,6,8],[5,7,8],[3,6,9],[0,1,9],[2,3,4],[2,5,7],[4,5,9],[0,7,8],[3,6,9],[1,4,9],[0,5,9],[3,7,8],[5,6,7],[2,3,6],[2,3,9],[0,1,6],[0,4,5],[1,4,5],[0,3,6]],[[0,3,9],[6,8,9],[0,3,6],[0,1,8],[1,7,9],[2,3,7],[0,2,9],[5,7,9],[0,2,9],[3,4,7],[1,5,9],[1,7,9],[1,6,7],[4,6,8],[1,4,6],[2,3,9],[0,3,6],[6,8,9],[0,3,8],[1,7,9],[4,8,9],[1,8,9],[1,2,5],[7,8,9],[0,1,7],[0,3,4],[0,4,8],[0,5,8],[0,3,7],[1,6,8],[1,7,8],[0,1,4],[0,4,9],[2,3,9],[3,5,7],[0,2,4],[0,1,8],[1,2,7],[3,6,7],[2,3,4],[0,4,8],[0,5,9],[3,6,9],[0,3,6],[0,7,8],[6,8,9],[0,2,6],[4,7,8],[4,5,8],[0,2,8],[0,2,7],[2,3,4],[4,5,7],[2,6,9],[1,3,5],[1,4,5],[0,4,8],[2,3,4],[4,5,8],[0,3,8],[2,7,9],[0,4,5],[2,3,5],[2,3,7],[3,4,6],[0,2,6],[1,3,5],[0,2,3],[1,2,4],[1,3,7],[0,2,8],[2,6,9],[6,7,8],[2,6,8],[0,4,6],[0,4,9],[0,3,8],[0,2,3],[1,3,4],[0,3,9],[1,2,8],[2,7,8],[2,4,9],[0,5,6],[0,3,5],[0,1,8],[1,2,4],[0,1,7],[0,3,9],[0,2,4],[2,3,7],[1,6,7],[0,7,9],[3,4,9],[3,4,8],[0,2,3],[6,7,8],[1,2,4],[1,2,7],[4,5,7],[2,3,8],[0,4,5],[2,5,9],[0,4,7],[0,7,8],[2,8,9],[2,5,7],[3,6,8],[0,2,5],[0,5,9],[1,8,9],[0,1,2],[0,2,7],[3,5,6],[5,8,9],[1,7,8],[0,3,9],[4,6,8],[0,1,6],[0,2,6],[6,7,8],[0,5,6],[3,6,7],[0,5,6],[2,4,5],[2,4,8],[5,7,8],[3,4,7],[1,8,9],[2,4,5],[0,6,9],[0,4,7],[0,2,9],[0,7,9],[1,7,8],[2,5,6],[4,5,8],[0,5,8],[0,3,4],[0,5,9],[1,2,9],[1,5,9],[2,6,7],[0,5,8],[3,4,6],[2,3,9],[1,2,7],[3,7,8],[0,2,4],[3,5,6],[4,8,9],[4,7,8],[2,6,9],[2,3,6],[7,8,9],[3,7,9],[1,4,8],[2,6,9],[0,1,7],[3,7,8],[7,8,9],[1,4,5],[0,2,8],[1,3,7],[6,7,8],[3,4,5],[1,5,6],[0,4,9],[0,3,9],[2,4,7],[1,2,9],[1,6,8],[1,3,8],[0,5,9],[5,7,9],[0,1,3],[2,4,5],[0,1,4],[3,6,9],[5,6,9],[3,4,5],[0,5,6],[4,7,9],[0,1,4],[0,2,5],[2,4,5],[4,5,9],[0,5,7],[4,7,9],[0,1,7],[0,3,6],[0,2,6],[5,7,8],[1,6,9],[4,6,8],[0,3,7],[1,5,9],[0,2,3],[2,4,8],[4,7,9],[3,4,8],[0,1,8],[0,8,9],[3,4,7],[3,4,8],[2,3,9],[2,5,8],[1,2,6],[4,6,8],[2,4,6],[0,3,8],[0,2,8],[4,6,7],[4,7,8],[2,3,6],[1,4,8],[1,3,5],[3,7,8],[0,5,7],[3,8,9],[0,8,9],[1,2,6],[0,1,9],[1,5,9],[1,3,6],[1,3,8],[1,4,9],[4,5,7],[6,8,9],[3,4,5],[0,7,8],[3,4,8],[0,6,7],[0,4,8],[1,3,9],[5,6,8],[1,4,9],[6,8,9],[0,3,7],[1,8,9],[1,7,8],[4,5,9],[4,6,9],[1,3,9],[2,3,4],[0,3,6],[1,8,9],[1,3,6],[1,3,4],[2,3,7],[0,4,7],[4,5,9],[1,4,8],[4,7,9],[0,1,4],[1,2,6],[0,4,5],[0,1,6],[3,5,6],[5,6,9],[2,6,8],[4,8,9],[0,1,4],[0,1,6],[0,4,8],[5,8,9],[4,5,7],[3,5,6],[0,2,9],[0,2,9],[1,4,7],[0,7,9],[0,2,5],[0,2,6],[0,1,4],[0,4,8],[0,5,7],[2,5,7],[0,1,8],[3,5,9],[4,5,6],[4,5,7],[2,6,7],[2,7,9],[2,4,5],[0,1,9],[0,6,8],[3,5,9],[3,6,7],[1,2,9],[3,4,7],[0,5,6],[2,7,8],[4,6,8],[0,2,7],[0,4,8],[2,7,9],[0,3,8],[1,6,7],[2,8,9],[5,6,9],[1,2,4],[1,2,8],[0,4,7],[1,3,5],[0,7,9],[4,5,7],[3,5,8],[2,5,7],[2,4,8],[1,2,8],[4,5,8],[3,7,8],[2,5,9],[2,5,9],[4,7,8],[1,2,9],[1,3,9],[1,6,7],[2,6,7],[5,6,9],[5,7,8],[3,5,9],[0,4,7],[1,2,6],[0,7,9],[0,1,3],[1,3,9],[3,7,9],[5,7,8],[0,6,8],[0,1,3],[0,4,6],[1,5,8],[1,6,8],[0,2,8],[2,5,6],[0,1,8],[4,7,8],[3,4,9],[1,3,9],[4,7,9],[3,5,7],[6,8,9],[1,5,8],[0,6,7],[1,2,6],[4,8,9],[0,1,9],[4,7,8],[2,5,9],[0,2,3],[0,3,4],[3,4,6],[0,5,6],[0,2,8],[3,7,8],[1,6,7],[3,5,7],[3,5,8],[1,5,8],[0,3,7],[0,2,6],[2,4,7],[0,6,7],[4,5,7],[1,3,8],[2,4,8],[2,3,9],[0,4,6],[1,4,5],[2,3,8],[1,4,6],[4,7,9],[4,5,9],[0,1,8],[0,2,7],[0,3,6],[6,7,9],[0,3,4],[3,4,8],[2,3,6],[0,3,8],[4,7,9],[5,8,9],[2,4,5],[1,3,4],[1,8,9],[1,5,9],[0,2,4],[1,6,7],[0,3,4],[4,6,8],[3,5,9],[1,3,9],[3,7,8],[2,5,6],[0,3,8],[1,5,6],[0,6,9],[5,7,9],[3,7,8],[5,6,7],[0,6,9],[5,7,8],[2,3,5],[0,1,6],[0,1,3],[0,2,6],[2,3,7],[1,2,4],[1,6,9],[1,4,7],[4,8,9],[1,4,5],[0,5,9],[4,6,8],[2,4,8],[4,6,9],[1,6,8],[2,7,9],[6,7,8],[1,4,9],[1,3,5],[0,4,8],[2,5,9],[3,4,8],[3,5,8],[6,7,9],[4,5,7],[2,5,9],[0,1,4],[5,7,9],[0,5,7],[5,8,9],[6,7,8],[2,5,6],[0,3,5],[0,4,7],[0,1,3],[1,2,9],[2,6,9],[1,2,7],[0,3,6],[3,4,7],[0,6,9],[0,2,4],[2,6,7],[0,6,8],[3,8,9],[3,4,5],[0,7,9],[5,8,9],[2,4,5],[0,2,8],[0,3,8],[0,3,4],[4,6,7],[0,1,8],[0,1,9],[1,6,7],[5,7,9],[1,6,7],[2,7,9],[5,6,9],[1,2,4],[0,6,8],[1,5,9],[1,3,6],[1,3,5],[4,6,8],[2,4,8],[3,4,6],[0,2,9],[4,5,7],[0,2,6],[2,3,4],[3,6,8],[2,5,8],[1,5,9],[5,7,9],[0,2,9],[0,4,7],[1,4,8],[2,4,7],[0,3,9],[2,4,7],[3,8,9],[3,5,8],[4,7,8],[1,2,3],[3,4,7],[1,2,4],[0,1,2],[3,5,8],[0,2,8],[0,4,8],[1,8,9],[0,6,7],[2,4,6],[2,3,6],[1,8,9],[0,2,7],[3,5,8],[0,4,8],[3,6,7],[0,3,6],[0,1,7],[2,4,9],[0,2,9],[0,4,8],[1,6,7]],[[1,4,8],[1,2,4],[0,2,4],[2,3,6],[1,3,7],[3,4,9],[1,2,3],[1,4,8],[2,3,4],[1,8,9],[2,4,7],[0,2,9],[0,6,8],[2,3,9],[0,3,5],[5,7,8],[0,2,3],[3,6,8],[1,6,8],[0,4,7],[4,8,9],[1,3,9],[0,4,9],[2,5,9],[0,2,5],[3,5,6],[2,4,7],[3,4,5],[0,1,6],[1,3,4],[1,2,7],[3,5,6],[2,4,8],[2,4,9],[3,5,8],[3,7,9],[2,5,9],[0,6,7],[0,6,8],[2,3,9],[2,5,8],[0,5,9],[1,4,7],[0,5,6],[5,7,9],[0,3,7],[0,3,4],[3,6,8],[5,8,9],[1,6,9],[0,2,5],[4,5,7],[1,3,6],[3,4,7],[0,8,9],[2,6,9],[4,8,9],[0,1,6],[0,4,5],[1,6,8],[0,1,8],[3,4,6],[1,3,4],[1,3,6],[1,2,3],[1,2,3],[6,8,9],[1,5,6],[1,4,6],[4,5,8],[1,6,9],[1,3,8],[0,3,8],[0,2,4],[1,2,6],[2,4,7],[1,4,6],[0,1,8],[0,5,9],[0,4,9],[2,3,4],[2,4,8],[0,7,9],[0,5,9],[5,7,8],[4,5,6],[0,1,6],[0,4,8],[0,1,5],[2,5,7],[3,4,6],[0,7,9],[0,5,9],[1,5,7],[3,7,8],[0,7,8],[0,1,5],[2,3,5],[1,8,9],[2,5,7],[4,5,8],[1,4,6],[3,7,9],[0,8,9],[1,5,9],[1,3,9],[0,8,9],[3,5,8],[0,5,8],[5,6,9],[1,3,7],[1,3,6],[0,4,5],[1,2,4],[1,3,5],[2,4,7],[0,8,9],[1,4,8],[1,5,7],[1,4,7],[0,6,7],[2,3,9],[2,4,6],[4,7,9],[0,6,9],[5,6,9],[0,2,3],[6,8,9],[3,5,7],[0,4,6],[0,6,8],[0,7,9],[2,5,9],[2,3,7],[0,2,3],[0,1,9],[1,4,9],[0,5,6],[0,2,8],[1,7,8],[0,2,5],[1,4,7],[1,2,9],[3,6,8],[0,6,7],[6,8,9],[2,4,6],[1,2,4],[3,6,8],[5,7,8],[0,5,8],[2,7,8],[0,2,5],[0,5,7],[0,3,8],[1,3,4],[0,2,9],[1,6,7],[0,3,4],[5,6,8],[0,3,8],[1,4,8],[0,5,9],[2,4,9],[0,7,9],[0,6,9],[2,3,5],[3,5,8],[2,3,9],[1,5,9],[6,7,9],[1,2,9],[1,6,7],[3,4,7],[1,2,5],[3,4,6],[0,8,9],[3,5,7],[0,4,7],[2,4,7],[3,7,9],[1,4,8],[3,4,6],[5,6,8],[4,5,8],[5,6,8],[2,4,6],[1,3,6],[0,2,9],[0,1,9],[3,5,7],[5,7,8],[0,5,8],[2,3,5],[2,5,6],[1,3,5],[1,4,9],[6,8,9],[0,1,5],[3,5,7],[1,6,9],[2,6,8],[0,1,6],[0,4,6],[5,7,8],[3,6,9],[1,2,7],[4,8,9],[5,8,9],[0,2,4],[2,4,9],[2,4,5],[0,3,9],[0,4,8],[1,4,6],[0,5,7],[2,5,6],[0,2,4],[2,4,8],[4,8,9],[4,8,9],[0,1,7],[0,1,6],[1,7,9],[3,6,9],[5,6,9],[1,2,3],[0,1,7],[2,8,9],[0,1,9],[6,8,9],[3,5,7],[0,3,5],[3,7,8],[3,5,7],[0,1,4],[1,2,4],[2,4,6],[4,6,9],[3,4,6],[0,1,7],[1,2,7],[5,6,7],[0,1,7],[6,7,8],[1,6,7],[3,4,9],[3,7,9],[0,5,9],[0,3,6],[2,4,5],[0,4,7],[1,2,3],[0,2,5],[2,4,6],[2,3,6],[0,2,5],[2,7,8],[1,2,7],[2,3,6],[1,6,7],[3,6,9],[0,6,9],[6,7,9],[0,4,7],[7,8,9],[0,5,8],[3,8,9],[2,7,8],[0,2,9],[4,6,9],[1,3,4],[1,5,9],[1,6,9],[2,3,4],[4,6,7],[2,3,6],[2,7,8],[2,4,5],[1,2,6],[0,1,3],[3,4,8],[2,7,8],[2,6,8],[6,8,9],[2,5,6],[1,3,5],[0,6,8],[2,3,7],[0,3,9],[2,8,9],[1,6,7],[2,6,9],[0,7,9],[2,5,6],[4,6,7],[0,2,8],[0,1,9],[1,5,7],[1,2,8],[4,8,9],[0,1,6],[2,6,9],[2,4,8],[3,7,9],[1,2,3],[0,2,7],[1,4,5],[1,6,9],[0,6,9],[1,2,6],[1,6,9],[1,2,9],[1,2,4],[4,5,6],[2,5,9],[3,4,9],[1,6,8],[2,4,9],[1,5,6],[0,3,7],[0,1,8],[0,2,4],[3,6,9],[6,8,9],[0,6,7],[3,4,9],[3,6,8],[4,8,9],[0,1,7],[4,5,9],[0,1,8],[0,3,9],[2,4,7],[0,2,9],[3,5,6],[1,5,9],[4,5,7],[0,4,9],[3,6,8],[3,5,7],[0,7,9],[2,8,9],[4,5,6],[1,2,9],[2,7,9],[1,4,7],[1,5,9],[0,6,9],[1,2,7],[2,7,9],[1,2,3],[5,7,8],[1,2,5],[5,7,9],[1,5,9],[1,7,9],[1,3,9],[4,5,7],[3,6,7],[2,5,7],[0,5,7],[2,5,9],[0,2,3],[0,3,9],[2,3,4],[0,3,9],[0,6,7],[1,4,9],[0,6,7],[1,4,7],[0,6,8],[5,8,9],[4,6,7],[3,6,9],[2,5,6],[1,3,8],[2,5,7],[1,7,8],[0,2,8],[1,5,9],[1,5,8],[3,6,7],[4,8,9],[4,6,7],[4,5,9],[1,2,8],[5,6,8],[0,4,6],[3,6,7],[6,7,8],[0,1,4],[1,2,8],[2,3,5],[6,8,9],[1,2,9],[0,2,5],[4,5,6],[5,6,8],[1,6,8],[0,5,8],[5,6,9],[0,5,6],[3,4,6],[1,5,6],[2,6,8],[0,3,6],[1,3,6],[3,5,7],[2,5,9],[3,5,8],[1,4,9],[0,5,8],[1,3,6],[1,4,6],[0,4,8],[0,6,7],[5,7,9],[0,5,9],[2,7,8],[3,7,9],[1,3,8],[2,3,9],[2,6,8],[0,7,9],[3,5,8],[0,4,6],[2,4,9],[1,5,7],[3,5,6],[2,3,9],[4,8,9],[1,5,9],[2,6,9],[1,3,8],[0,7,8],[2,7,8],[1,3,5],[0,6,7],[2,5,6],[0,2,7],[5,6,8],[1,6,9],[0,1,4],[3,7,9],[1,6,8],[1,4,9],[2,3,8],[4,5,8],[0,1,4],[0,4,7],[1,4,9],[4,5,6],[0,5,6],[1,6,7],[0,5,9],[1,3,4],[0,6,9],[3,4,8],[1,7,9],[1,4,7],[1,6,8],[3,4,7],[0,1,9],[6,7,9],[4,5,8],[3,5,9],[0,6,8],[1,6,7],[1,4,5],[2,6,7],[1,4,8],[0,5,9],[3,7,9],[0,6,7],[0,2,5],[3,7,8],[3,6,7],[3,6,9],[4,5,9],[5,6,8],[0,2,7],[2,4,6],[2,5,8],[0,6,9],[2,4,7],[2,6,9],[3,5,7],[1,6,9],[4,8,9],[2,6,8],[3,8,9],[0,1,3],[2,3,7],[0,5,7],[0,2,3],[1,4,9],[0,2,3],[4,8,9],[1,3,7],[5,7,8],[4,8,9],[7,8,9],[5,6,8],[1,2,9],[0,1,8],[2,3,6],[3,5,8],[0,5,7],[3,4,9],[4,5,7],[0,2,7]],[[3,7,8],[0,2,8],[7,8,9],[2,5,7],[4,5,9],[0,5,8],[0,1,9],[1,5,6],[1,4,5],[6,8,9],[0,3,9],[1,2,8],[1,3,4],[2,8,9],[0,3,6],[0,3,4],[2,4,9],[0,2,3],[2,8,9],[2,3,8],[2,3,5],[1,3,6],[5,6,7],[0,1,3],[2,3,7],[4,6,8],[5,6,8],[2,6,9],[0,3,6],[1,4,8],[3,4,9],[1,4,9],[0,5,7],[1,3,7],[1,2,8],[0,8,9],[0,6,8],[0,8,9],[0,1,4],[0,3,8],[0,1,7],[0,4,5],[1,6,9],[0,4,9],[1,8,9],[0,6,9],[1,2,7],[1,4,5],[1,4,9],[2,4,7],[1,3,8],[0,3,6],[0,2,4],[3,7,8],[4,8,9],[0,3,6],[0,2,8],[2,3,4],[0,1,3],[2,4,8],[0,7,9],[0,6,9],[0,2,3],[1,2,5],[1,2,4],[5,7,8],[0,3,9],[0,7,8],[0,4,9],[0,1,2],[0,3,6],[0,1,9],[1,2,9],[4,5,9],[6,8,9],[5,6,7],[1,4,6],[4,7,9],[0,3,8],[2,3,6],[1,3,7],[4,8,9],[2,4,9],[1,2,6],[0,3,6],[2,4,7],[5,7,9],[2,3,9],[0,5,6],[4,7,9],[5,6,9],[1,5,7],[2,6,7],[1,7,9],[0,3,4],[1,6,9],[0,6,7],[5,6,7],[0,5,8],[4,5,9],[0,1,3],[3,8,9],[0,1,7],[0,5,6],[6,8,9],[2,5,6],[0,6,7],[0,5,9],[1,2,9],[0,2,4],[0,3,5],[0,3,9],[1,5,9],[2,7,8],[0,6,9],[1,5,6],[0,5,8],[6,8,9],[0,5,7],[1,8,9],[1,2,8],[2,6,7],[0,4,8],[1,6,9],[2,4,5],[5,7,9],[2,4,9],[3,4,6],[0,1,4],[4,5,6],[0,8,9],[0,5,7],[3,5,8],[2,3,4],[0,3,9],[2,4,6],[0,3,6],[2,4,6],[0,7,9],[0,6,7],[3,4,9],[2,3,5],[1,5,6],[2,3,7],[2,5,8],[2,7,8],[4,5,9],[0,8,9],[6,7,8],[2,8,9],[1,4,8],[1,5,7],[2,4,9],[2,4,9],[2,6,9],[0,4,5],[0,5,8],[2,3,4],[0,6,9],[2,3,5],[7,8,9],[3,4,9],[3,6,7],[1,7,9],[1,3,7],[1,5,8],[2,6,8],[1,5,8],[1,4,7],[1,3,6],[0,5,8],[1,3,8],[5,7,9],[1,2,5],[0,3,5],[5,7,9],[6,7,8],[1,4,5],[1,2,5],[5,8,9],[4,7,8],[3,4,9],[3,4,7],[0,1,3],[3,4,7],[0,6,8],[2,6,9],[1,2,8],[1,6,9],[0,5,8],[0,4,7],[1,8,9],[2,6,8],[0,1,5],[0,6,8],[0,2,7],[3,4,5],[0,5,6],[2,6,7],[1,6,7],[0,1,3],[1,8,9],[1,4,6],[1,2,6],[0,2,6],[2,8,9],[1,5,6],[3,4,9],[0,2,9],[0,4,7],[0,1,3],[0,5,7],[0,6,8],[3,8,9],[3,7,9],[4,7,9],[0,4,9],[2,3,7],[5,6,7],[1,3,7],[0,3,6],[4,5,8],[5,6,7],[3,7,8],[0,7,9],[2,7,9],[1,5,6],[2,3,5],[2,7,8],[3,4,5],[4,5,9],[1,3,4],[6,7,9],[4,5,6],[2,8,9],[2,4,9],[4,5,6],[0,1,8],[2,5,8],[4,7,8],[0,1,3],[1,2,3],[0,3,5],[0,2,6],[3,8,9],[3,5,8],[5,6,8],[0,2,3],[3,4,7],[1,6,9],[0,1,5],[4,5,7],[1,7,9],[6,8,9],[2,7,8],[2,6,7],[1,5,9],[3,5,8],[3,6,9],[1,3,8],[0,1,7],[3,4,8],[1,3,7],[0,2,4],[0,2,4],[4,6,7],[0,1,6],[4,6,8],[0,1,6],[4,5,7],[1,2,6],[1,4,9],[0,5,7],[1,2,6],[0,6,9],[0,4,7],[0,2,9],[1,3,6],[3,5,6],[0,4,5],[1,3,4],[1,2,5],[1,3,6],[2,5,8],[0,3,5],[2,7,8],[0,3,9],[1,6,9],[2,6,8],[1,4,5],[1,4,7],[1,4,8],[0,3,8],[2,7,9],[0,3,7],[0,1,6],[0,1,8],[1,6,9],[1,2,9],[1,4,9],[0,6,7],[7,8,9],[2,3,5],[1,4,9],[2,7,8],[0,2,9],[0,3,7],[0,6,9],[0,4,9],[4,6,8],[0,2,9],[2,4,8],[3,4,9],[1,5,8],[4,7,9],[2,3,7],[0,2,9],[2,4,6],[0,1,6],[0,1,9],[2,6,8],[1,8,9],[0,8,9],[1,5,6],[1,6,8],[1,8,9],[0,3,8],[2,4,9],[3,7,8],[0,2,3],[1,2,7],[0,1,5],[2,4,9],[1,3,5],[2,3,6],[0,3,7],[0,2,7],[2,3,6],[3,4,7],[3,7,9],[2,5,9],[1,5,8],[4,7,8],[2,4,6],[1,2,9],[3,5,7],[1,2,3],[3,4,7],[0,8,9],[1,4,8],[2,8,9],[2,4,6],[2,4,6],[3,5,8],[5,8,9],[2,4,6],[3,6,9],[0,6,7],[1,3,9],[1,3,8],[3,4,8],[2,3,5],[3,8,9],[1,5,7],[0,7,9],[2,3,5],[1,4,6],[3,5,9],[1,6,9],[2,4,8],[2,7,9],[2,3,8],[2,5,6],[3,4,5],[1,6,9],[0,7,8],[0,7,8],[2,3,9],[3,7,9],[0,6,7],[1,7,8],[0,2,6],[5,6,7],[3,4,5],[0,6,7],[1,7,8],[1,2,3],[1,3,8],[3,6,8],[1,6,7],[1,3,9],[6,8,9],[2,7,9],[3,4,7],[0,2,3],[0,6,7],[1,5,8],[3,6,9],[1,4,7],[1,8,9],[2,6,8],[0,5,9],[2,8,9],[4,7,9],[1,5,6],[0,1,5],[5,7,8],[5,7,9],[3,5,8],[1,3,5],[2,3,9],[0,5,6],[2,4,8],[4,6,9],[2,5,8],[2,4,9],[2,3,7],[2,3,4],[0,2,7],[1,7,8],[0,5,9],[0,5,6],[1,7,8],[0,7,8],[2,6,9],[2,4,5],[0,1,8],[6,8,9],[4,5,8],[7,8,9],[1,5,9],[6,7,8],[1,2,7],[0,2,9],[2,3,9],[2,3,4],[0,3,8],[0,4,7],[2,5,8],[0,6,8],[1,4,6],[0,1,2],[4,5,9],[1,3,9],[4,8,9],[4,8,9],[0,1,6],[1,2,4],[1,5,7],[1,3,5],[1,3,7],[0,3,5],[0,3,6],[1,3,6],[2,5,6],[2,3,9],[6,8,9],[5,6,9],[2,4,9],[3,6,9],[5,8,9],[4,8,9],[2,3,6],[2,3,4],[3,4,6],[3,8,9],[1,2,8],[5,7,8],[0,3,7],[0,1,6],[2,3,6],[1,4,8],[1,4,7],[4,6,7],[1,4,6],[0,8,9],[2,7,9],[0,3,8],[1,2,4],[3,4,6],[0,2,7],[1,5,7],[2,3,4],[1,6,7],[2,5,7],[4,6,8],[1,2,9],[5,8,9],[1,4,6],[1,8,9],[0,3,8],[2,4,6],[1,4,6],[0,5,7],[4,8,9],[0,4,9],[0,4,5],[1,5,6],[0,4,8],[0,5,9],[3,6,8],[0,6,7],[2,3,9],[2,4,5],[0,3,5],[1,8,9],[3,4,8],[4,6,7],[1,2,3],[1,6,8],[2,3,8],[5,6,7]],[[0,6,8],[2,5,6],[4,6,7],[2,4,9],[0,1,5],[2,5,9],[2,3,8],[1,2,5],[0,1,7],[1,2,5],[1,5,6],[1,6,8],[6,8,9],[2,3,6],[2,4,7],[0,2,8],[3,4,8],[4,5,8],[3,4,9],[0,5,8],[2,5,6],[0,1,8],[2,5,8],[0,8,9],[1,2,6],[2,3,8],[0,3,9],[1,3,9],[0,2,5],[2,4,5],[2,5,8],[1,4,8],[1,4,6],[0,5,6],[0,3,8],[0,1,5],[1,5,9],[1,3,6],[1,5,8],[4,6,8],[0,1,8],[3,7,9],[2,5,7],[0,3,5],[0,1,2],[2,7,9],[3,6,8],[2,5,6],[0,3,8],[1,8,9],[1,3,4],[0,1,6],[1,3,6],[3,5,7],[3,5,7],[0,2,3],[0,1,7],[0,4,9],[3,5,8],[0,1,3],[0,5,9],[0,2,9],[1,5,8],[2,3,7],[1,4,5],[2,4,9],[3,6,7],[1,5,6],[0,1,4],[3,6,7],[4,6,9],[2,3,5],[5,6,8],[1,6,8],[0,2,6],[1,3,4],[2,3,6],[0,1,2],[5,7,8],[0,5,8],[1,2,4],[1,2,5],[1,3,9],[0,3,8],[0,3,6],[0,5,9],[1,4,8],[0,4,9],[1,6,8],[0,2,4],[0,6,8],[1,5,8],[1,2,5],[0,3,4],[2,5,6],[3,4,8],[0,2,9],[1,3,8],[0,5,6],[0,5,6],[0,1,5],[0,6,9],[3,4,9],[6,7,8],[3,7,8],[0,1,2],[2,5,6],[3,5,9],[0,1,4],[3,5,8],[1,3,9],[0,6,8],[0,2,6],[0,1,6],[5,7,9],[5,6,8],[0,4,5],[1,3,8],[2,6,7],[1,4,7],[2,5,6],[1,3,4],[2,3,8],[1,6,9],[1,6,8],[0,5,9],[2,5,6],[1,2,6],[3,4,8],[0,3,6],[0,3,8],[6,7,9],[1,3,4],[2,4,7],[3,5,9],[0,7,9],[5,6,7],[1,3,8],[2,7,8],[1,5,7],[1,5,9],[5,7,8],[3,7,9],[2,4,8],[2,3,4],[0,4,5],[1,2,7],[2,3,5],[4,5,7],[5,7,8],[1,4,5],[1,4,5],[3,5,6],[1,5,9],[0,4,8],[3,4,7],[0,3,6],[2,3,8],[3,4,6],[0,6,9],[0,7,8],[1,7,9],[3,5,6],[4,5,6],[4,5,6],[4,6,9],[6,7,9],[4,5,7],[1,2,6],[1,4,9],[1,5,8],[5,6,8],[1,5,9],[4,5,8],[3,8,9],[1,2,6],[3,5,8],[4,8,9],[2,4,6],[3,5,9],[1,2,8],[2,3,5],[2,4,9],[2,4,9],[2,5,6],[1,3,4],[2,4,5],[3,5,6],[0,7,9],[0,3,4],[1,2,8],[0,3,4],[3,4,6],[0,2,6],[1,8,9],[2,4,9],[3,4,8],[3,6,8],[2,5,8],[0,6,7],[0,5,9],[2,3,7],[0,1,6],[2,3,8],[2,3,5],[3,4,7],[2,4,9],[6,7,8],[0,2,3],[1,6,8],[0,4,5],[2,3,5],[4,5,6],[3,6,8],[3,5,6],[1,5,8],[0,2,8],[2,6,9],[0,3,6],[0,3,9],[0,1,2],[0,8,9],[2,3,6],[3,5,6],[1,2,9],[1,4,6],[0,4,5],[1,3,5],[1,4,9],[7,8,9],[1,3,5],[0,3,4],[0,3,9],[0,3,4],[0,1,2],[5,6,9],[5,7,9],[1,2,6],[2,3,4],[1,8,9],[4,6,7],[1,4,9],[3,5,6],[4,6,7],[1,2,8],[6,8,9],[1,7,9],[1,6,9],[5,8,9],[0,4,8],[3,4,9],[2,4,6],[0,2,6],[0,5,7],[0,1,2],[0,8,9],[0,2,5],[2,7,8],[3,4,6],[5,6,7],[6,7,9],[3,6,8],[1,5,7],[0,4,9],[2,6,8],[2,5,9],[0,6,9],[2,7,9],[4,5,9],[1,2,4],[0,3,8],[1,3,8],[1,8,9],[2,4,7],[2,6,7],[2,5,7],[2,7,9],[4,5,6],[2,4,6],[1,7,8],[0,5,9],[1,2,6],[1,4,9],[3,5,7],[3,4,5],[2,8,9],[3,4,9],[1,3,5],[0,3,8],[0,3,5],[2,5,9],[0,1,2],[1,4,5],[2,4,5],[0,3,8],[4,8,9],[1,5,8],[0,1,6],[5,6,8],[1,4,9],[6,7,8],[1,7,9],[1,5,7],[6,7,8],[4,6,9],[2,5,6],[0,5,6],[3,7,9],[1,6,9],[4,5,9],[1,2,5],[1,3,9],[1,2,5],[5,7,9],[1,4,9],[3,4,8],[1,5,7],[0,4,8],[1,5,6],[0,2,4],[2,4,9],[4,6,7],[4,7,8],[4,6,8],[5,7,8],[0,7,8],[4,8,9],[6,8,9],[1,3,7],[3,5,8],[3,5,9],[2,4,8],[3,6,9],[0,2,5],[5,7,9],[0,2,3],[0,2,8],[1,3,9],[3,4,7],[0,7,8],[3,4,8],[0,8,9],[0,2,6],[1,3,9],[3,8,9],[1,6,9],[1,5,9],[1,2,5],[0,1,7],[3,5,7],[0,2,9],[2,4,6],[1,6,9],[1,7,9],[5,6,8],[6,8,9],[0,3,7],[1,5,8],[0,5,7],[5,7,9],[0,1,7],[1,4,9],[2,6,7],[5,8,9],[4,5,6],[0,2,7],[0,3,7],[1,2,6],[0,3,8],[1,4,5],[0,1,2],[3,7,9],[4,5,7],[0,3,5],[3,6,9],[2,4,9],[0,2,7],[4,6,7],[3,4,9],[0,3,8],[3,4,5],[0,4,9],[0,3,4],[3,5,6],[1,6,8],[0,3,7],[1,4,8],[3,4,9],[1,3,5],[4,7,9],[3,5,7],[1,5,6],[0,6,8],[3,4,5],[0,4,9],[3,4,6],[0,4,5],[0,1,9],[5,6,8],[4,5,9],[0,4,8],[0,1,7],[5,6,8],[1,3,4],[3,5,7],[0,7,9],[2,3,7],[2,8,9],[0,5,9],[2,5,6],[1,8,9],[0,2,4],[1,7,8],[0,7,9],[3,4,9],[0,3,4],[3,4,5],[3,8,9],[0,5,6],[1,5,8],[5,6,8],[1,4,6],[5,6,9],[5,6,8],[2,7,9],[0,1,5],[2,3,9],[0,1,4],[2,3,4],[2,5,7],[2,4,9],[1,8,9],[1,7,8],[4,5,6],[1,3,6],[1,3,5],[1,6,9],[1,4,9],[1,7,9],[1,2,7],[1,4,7],[3,4,6],[3,4,9],[0,1,6],[1,5,6],[0,2,8],[2,4,6],[0,1,3],[2,7,9],[0,6,7],[1,4,6],[0,2,3],[1,5,7],[0,6,9],[3,6,9],[1,4,8],[2,3,8],[1,2,3],[0,3,5],[0,5,7],[5,8,9],[1,5,8],[5,6,8],[6,7,9],[5,7,8],[0,4,7],[5,8,9],[2,3,9],[1,7,9],[1,2,7],[4,8,9],[0,1,6],[0,8,9],[0,6,8],[3,5,8],[3,6,8],[2,5,7],[1,2,8],[0,4,9],[0,2,4],[0,3,9],[2,4,7],[2,4,6],[1,3,7],[5,6,9],[0,5,9],[1,2,8],[4,5,7],[3,5,7],[1,6,8],[1,3,8],[2,4,9],[5,8,9],[5,8,9],[1,2,3],[1,2,7],[7,8,9],[0,2,3],[3,7,8],[1,3,5],[2,6,8],[4,5,9],[6,8,9],[3,4,9],[3,5,8],[3,4,8],[0,6,9],[0,1,3],[0,3,4],[3,5,6],[4,5,8],[1,3,7]]]
def setup_inputs(rng):
    return {"x": rng.standard_normal((N, 128, TOK), dtype=np.float32).astype(ml_dtypes.bfloat16), "gate": (0.5 * rng.integers(1, 4, size=(N, K, TOK)) * (2 * rng.integers(0, 2, size=(N, K, TOK)) - 1)).astype(np.float32).astype(ml_dtypes.bfloat16), "w1": (rng.standard_normal((N, 128, FT * 128), dtype=np.float32) / 8).astype(ml_dtypes.bfloat16), "w2": (rng.standard_normal((N, 128, FT * 128), dtype=np.float32) / 8).astype(ml_dtypes.bfloat16)}
def setup_inputs_big(rng):
    d = setup_inputs(rng)
    for k in ("x", "gate", "w1", "w2"): d[k] = (d[k].astype(np.float32) * 1024.0).astype(d[k].dtype)
    return d
def setup_inputs_small(rng):
    d = setup_inputs(rng)
    for k in ("x", "gate", "w1", "w2"): d[k] = (d[k].astype(np.float32) * (1 / 1024.0)).astype(d[k].dtype)
    return d
def reference(x, gate, w1, w2):
    X, GATE, W1, W2 = x.astype(np.float64), gate.astype(np.float64), w1.astype(np.float64), w2.astype(np.float64)
    y = np.zeros((N, 128, TOK))
    for r in range(N):
        for t in range(TOK):
            for i, e in enumerate(ROUTE[r][t]):
                hid = np.maximum(W1[e].T @ X[r][:, t], 0.0)
                y[r][:, t] += GATE[r][i, t] * sum(W2[e][:, 128 * f:128 * f + 128].T @ hid[128 * f:128 * f + 128] for f in range(FT))
    return {"y": y.astype(ml_dtypes.bfloat16)}

@@ -1,0 +1,282 @@
+from concourse.bass import DstId, RemoteDMATransfer
+from concourse.mybir import AluOpType
+
+NSIM = 80
+NX = 10
+TOKS = 512
+BLK = 128
+PRE = 5
+
+SCRATCH = {
+    "wall": ("sbuf", [128, NX * 256], "bfloat16"),
+    "xs": ("sbuf", [128, TOKS], "bfloat16"),
+    "zeros": ("sbuf", [128, TOKS], "bfloat16"),
+    "r": ("sbuf", [128, NX * TOKS], "bfloat16"),
+    "rg": ("sbuf", [128, NX * TOKS], "bfloat16"),
+    "grep": ("sbuf", [128, TOKS], "bfloat16"),
+    "mks": ("sbuf", [128, TOKS], "bfloat16"),
+    "gs": ("sbuf", [128, TOKS], "bfloat16"),
+    "sel": ("sbuf", [128, NX * 128], "bfloat16"),
+    "ysb": ("sbuf", [128, TOKS], "bfloat16"),
+    "seed": ("sbuf", [128, 129], "bfloat16"),
+    "eye": ("dram", [129, 128, 1], "bfloat16"),
+    "mk": ("dram", [3 * NX * 4, 128, 1], "bfloat16"),
+    "h0": ("psum", [128, 512], "float32"),
+    "h1": ("psum", [128, 512], "float32"),
+    "h2": ("psum", [128, 512], "float32"),
+    "g0": ("psum", [128, 512], "float32"),
+    "g1": ("psum", [128, 512], "float32"),
+    "g2": ("psum", [128, 512], "float32"),
+    "ya": ("psum", [128, 512], "float32"),
+    "yb": ("psum", [128, 512], "float32"),
+}
+SEMAPHORES = ["wl", "xl", "gl", "ml", "marr", "sent", "st", "fs", "tl", "hs", "rs", "gsd", "gq", "ms",
+              "yqa", "yqb", "ca", "cb"] + ["wa%d" % e for e in range(NX)]
+
+
+def _bits(m):
+    return [1 << b for b in range(16) if (m >> b) & 1]
+
+
+def _rows(route_r, kslots):
+    rows, span = [], {}
+    for e in range(NX):
+        sl = [i for i in range(kslots) if any(tok[i] == e for tok in route_r)]
+        if not sl:
+            continue
+        i0, i1 = min(sl), max(sl) + 1
+        span[e] = (len(rows), len(rows) + i1 - i0, i0, i1)
+        for i in range(i0, i1):
+            rows.append((e, i))
+    return rows, span
+
+
+def _builder(g, core, T, topo, rank, which, nbuild):
+    route_r = T.tables["ROUTE"][rank]
+    rows, _ = _rows(route_r, T.tables["K"])
+    dst = T.cores[rank]
+    rid, pid, _se = topo.addr(dst)
+    eng = _bits(topo.mask(core, dst))
+    pieces = []
+    for k, (e, i) in enumerate(rows):
+        for b in range(TOKS // BLK):
+            src = [j for j in range(BLK) if route_r[b * BLK + j][i] == e]
+            pieces.append((len(src), 4 * k + b, src))
+    pieces.sort(key=lambda p: (-p[0], p[1]))
+    mine = pieces[which::nbuild]
+    ne = len(eng)
+    calls = [mine[a:a + ne] for a in range(0, len(mine), ne)]
+    g.vector.memset(T.seed[:, 0:1], 1.0).then_inc(T.sem.fs, 1)
+    g.vector.memset(T.seed[:, 1:129], 0.0).then_inc(T.sem.fs, 1)
+    g.sync.wait_ge(T.sem.fs, 2)
+    g.sync.dma_start(T.eye[:], T.seed[:]).then_inc(T.sem.tl, 16)
+    g.wait_ge(T.sem.tl, 16)
+    total = 0
+    for ci, call in enumerate(calls):
+        if ci % 2:
+            call = call[::-1]
+        trs = []
+        for q, (_n, slot, src) in enumerate(call):
+            ids = list(src)
+            while len(ids) < 2:
+                ids.append(128)
+            if len(ids) > 64:
+                raise ValueError("a fold takes at most 64 sources")
+            trs.append(RemoteDMATransfer(dst_ids=[DstId(rid=rid, pnc=pid)], dma_engine_mask=eng[q],
+                                         remote_sem=T.sem.marr, srcs=[T.eye[j] for j in ids],
+                                         dsts=[T.mk[slot]], alu_op=1))
+            total += 1
+        g.remote_dma_fused(trs, local_sem=T.sem.sent)
+    g.wait_ge(T.sem.sent, total)
+
+
+def rank_program(g, core, T, topo):
+    cores = list(T.cores)
+    rank = T.rank_of(core)
+    if rank is None:
+        for r, rc in enumerate(cores):
+            if topo.chip(rc) == topo.chip(core) and topo.die(rc) == topo.die(core):
+                team = [c for c in range(NSIM) if c not in cores
+                        and topo.chip(c) == topo.chip(rc) and topo.die(c) == topo.die(rc)]
+                _builder(g, core, T, topo, r, team.index(core), len(team))
+                return
+        return
+
+    S = T.sem
+    route_r = T.tables["ROUTE"][rank]
+    rows, span = _rows(route_r, T.tables["K"])
+    KR = len(rows)
+
+    chips = sorted(set(topo.chip(c) for c in cores))
+    nch = len(chips)
+    me = chips.index(topo.chip(core))
+
+    def on_chip(ch):
+        return [r for r, c in enumerate(cores) if topo.chip(c) == ch]
+
+    def port_rank(ch, sender):
+        rs = on_chip(ch)
+        same = [r for r in rs if topo.die(cores[r]) == topo.die(cores[sender])]
+        return same[0] if same else rs[0]
+
+    mates = [r for r in on_chip(chips[me]) if r != rank]
+    out_peers = [port_rank(chips[(me + k) % nch], rank) for k in range(1, nch)]
+    direct, fwd = [], []
+    for k in range(1, nch):
+        for s in on_chip(chips[(me - k) % nch]):
+            (direct if port_rank(chips[me], s) == rank else fwd).append(s)
+    off_mask = topo.mask(core, cores[out_peers[0]])
+    on_mask = topo.mask(core, cores[mates[0]])
+    up = on_mask & ~off_mask
+    if len(_bits(up)) not in (1, 2, 4, 8, 16):
+        up = on_mask
+    n_off, n_on = len(_bits(off_mask)), len(_bits(up))
+    arrive = {}
+    for s in direct:
+        arrive[s] = n_off
+    for s in fwd + mates:
+        arrive[s] = n_on
+
+    order = [rank] + mates + direct[:3] + fwd[:1] + direct[3:4] + fwd[1:] + direct[4:]
+    order = [e for e in order if e in span]
+    NQ = len(order)
+    last = NQ - 1
+    pre = min(PRE, NQ)
+
+    def wslot(e):
+        return T.wall[:, 256 * e:256 * e + 256]
+
+    g.sync.dma_start(T.wall[:, 256 * rank:256 * rank + 128], T.w1[:, :]).then_inc(S.wl, 16)
+    g.scalar.dma_start(T.wall[:, 256 * rank + 128:256 * rank + 256], T.w2[:, :]).then_inc(S.wl, 16)
+    g.sync.dma_start(T.xs[:], T.x[:, :]).then_inc(S.xl, 16)
+    ngl = 0
+    for n, e in enumerate(sorted(span)):
+        k0, k1, i0, i1 = span[e]
+        q = g.scalar if n % 2 == 0 else g.sync
+        q.dma_start(T.grep[k0:k1, :], T.gate[i0:i1, :]).then_inc(S.gl, 16)
+        ngl += 16
+    g.sync.wait_ge(S.marr, 4 * KR)
+    g.sync.dma_start(T.mks[0:KR, :], T.mk[0:4 * KR]).then_inc(S.ml, 16)
+
+    nsent = 0
+
+    def send(e, dst_rank, mask):
+        rid, pid, _se = topo.addr(cores[dst_rank])
+        g.remote_dma(out_ap=wslot(e), in_ap=wslot(e), remote_sem=S["wa%d" % e], local_sem=S.sent,
+                     pid=pid, routing_id=rid, dma_engine_mask=mask)
+        return len(_bits(mask))
+
+    g.wait_ge(S.wl, 32)
+    nsent += send(rank, out_peers[0], off_mask)
+    for m in mates:
+        nsent += send(rank, m, up)
+    for p in out_peers[1:]:
+        nsent += send(rank, p, off_mask)
+    for s in direct:
+        g.wait_ge(S["wa%d" % s], arrive[s])
+        for m in mates:
+            nsent += send(s, m, up)
+
+    H = [T.h0, T.h1, T.h2]
+    GB = [T.g0, T.g1, T.g2]
+    YP = [T.ya, T.yb]
+    YQ = [S.yqa, S.yqb]
+    nfill = 2 + len(span) + len([e for e in span if span[e][0] > 0])
+    te, ve = g.tensor, g.vector
+
+    def mm_h(n):
+        e = order[n]
+        if e == rank:
+            te.wait_ge(S.wl, 32)
+        else:
+            te.wait_ge(S["wa%d" % e], arrive[e])
+        if n == 0:
+            te.wait_ge(S.xl, 16)
+        if n >= 3:
+            te.wait_ge(S.rs, n - 2)
+        te.matmul(out=H[n % 3][:], lhsT=T.wall[:, 256 * e:256 * e + 128], rhs=T.xs[:],
+                  start=True, stop=True).then_inc(S.hs, 1)
+
+    def mm_g(n):
+        e = order[n]
+        if n == 0:
+            te.wait_ge(S.fs, nfill)
+            te.wait_ge(S.gsd, 1)
+        if n >= 3:
+            te.wait_ge(S.ms, 2 * (n - 2))
+        te.matmul(out=GB[n % 3][:], lhsT=T.sel[0:KR, 128 * e:128 * e + 128], rhs=T.gs[0:KR, :],
+                  start=True, stop=True).then_inc(S.gq, 1)
+
+    def mm_y(n):
+        e = order[n]
+        for a in range(2):
+            te.wait_ge(S.ms, 2 * n + 2 if n < last else 2 * n + 1 + a)
+            te.matmul(out=YP[a][:, 0:256], lhsT=T.wall[:, 256 * e + 128:256 * e + 256],
+                      rhs=T.rg[:, 512 * n + 256 * a:512 * n + 256 * a + 256],
+                      start=(n == 0), stop=(n == last)).then_inc(YQ[a], 1)
+
+    for n in range(pre):
+        mm_h(n)
+    for n in range(min(3, NQ)):
+        mm_g(n)
+    for n in range(NQ):
+        if pre + n < NQ:
+            mm_h(pre + n)
+        mm_y(n)
+        if n + 3 < NQ:
+            mm_g(n + 3)
+
+    ve.memset(T.zeros[:], 0.0).then_inc(S.fs, 1)
+    ve.memset(T.sel[0:KR, :], 0.0).then_inc(S.fs, 1)
+    ve.wait_ge(S.fs, 2)
+    nf = 2
+    for e in sorted(span):
+        ve.memset(T.sel[0:span[e][1], 128 * e:128 * e + 128], 1.0).then_inc(S.fs, 1)
+        nf += 1
+    ve.wait_ge(S.fs, nf)
+    for e in sorted(span):
+        if span[e][0] > 0:
+            ve.memset(T.sel[0:span[e][0], 128 * e:128 * e + 128], 0.0).then_inc(S.fs, 1)
+            nf += 1
+
+    def relu(n):
+        ve.wait_ge(S.hs, n + 1)
+        ve.tensor_tensor(out=T.r[:, 512 * n:512 * n + 512], in0=H[n % 3][:], in1=T.zeros[:],
+                         op=AluOpType.max).then_inc(S.rs, 1)
+
+    def gatemul(n):
+        ve.wait_ge(S.gq, n + 1)
+        ve.wait_ge(S.rs, n + 1)
+        if n < last:
+            ve.tensor_tensor(out=T.rg[:, 512 * n:512 * n + 512], in0=T.r[:, 512 * n:512 * n + 512],
+                             in1=GB[n % 3][:], op=AluOpType.mult).then_inc(S.ms, 2)
+        else:
+            for a in range(2):
+                c = 512 * n + 256 * a
+                ve.tensor_tensor(out=T.rg[:, c:c + 256], in0=T.r[:, c:c + 256],
+                                 in1=GB[n % 3][:, 256 * a:256 * a + 256], op=AluOpType.mult).then_inc(S.ms, 1)
+
+    for n in range(pre):
+        relu(n)
+    ve.wait_ge(S.gl, ngl)
+    ve.wait_ge(S.ml, 16)
+    ve.tensor_tensor(out=T.gs[0:KR, :], in0=T.mks[0:KR, :], in1=T.grep[0:KR, :],
+                     op=AluOpType.mult).then_inc(S.gsd, 1)
+    for n in range(NQ):
+        if pre + n < NQ:
+            relu(pre + n)
+        gatemul(n)
+    CS = [S.ca, S.cb]
+    for a in range(2):
+        ve.wait_ge(YQ[a], NQ)
+        ve.tensor_copy(out=T.ysb[:, 256 * a:256 * a + 256], in_=YP[a][:, 0:256]).then_inc(CS[a], 1)
+
+    for a, q in enumerate((g.sync, g.scalar)):
+        q.wait_ge(CS[a], 1)
+        q.dma_start(T.y[:, 256 * a:256 * a + 256], T.ysb[:, 256 * a:256 * a + 256]).then_inc(S.st, 16)
+
+    g.wait_ge(S.sent, nsent)
+    for e in range(NX):
+        if e != rank:
+            g.wait_ge(S["wa%d" % e], arrive[e])
+    g.wait_ge(S.st, 32)

@@ -5,22 +5,24 @@ NSIM = 80
 NX = 10
 TOKS = 512
 BLK = 128
-PRE = 5
+NH = 3
 
 SCRATCH = {
     "wall": ("sbuf", [128, NX * 256], "bfloat16"),
     "xs": ("sbuf", [128, TOKS], "bfloat16"),
     "zeros": ("sbuf", [128, TOKS], "bfloat16"),
-    "r": ("sbuf", [128, NX * TOKS], "bfloat16"),
-    "rg": ("sbuf", [128, NX * TOKS], "bfloat16"),
+    "r": ("sbuf", [128, 4 * TOKS], "bfloat16"),
+    "rg": ("sbuf", [128, 4 * TOKS], "bfloat16"),
     "grep": ("sbuf", [128, TOKS], "bfloat16"),
     "mks": ("sbuf", [128, TOKS], "bfloat16"),
     "gs": ("sbuf", [128, TOKS], "bfloat16"),
-    "sel": ("sbuf", [128, NX * 128], "bfloat16"),
+    "sel": ("sbuf", [128, 4 * 128], "bfloat16"),
     "ysb": ("sbuf", [128, TOKS], "bfloat16"),
+    "part": ("sbuf", [128, NH * TOKS], "bfloat16"),
     "seed": ("sbuf", [128, 129], "bfloat16"),
     "eye": ("dram", [129, 128, 1], "bfloat16"),
-    "mk": ("dram", [3 * NX * 4, 128, 1], "bfloat16"),
+    "mk": ("dram", [3 * 4 * 4, 128, 1], "bfloat16"),
+    "gd": ("dram", [3, 128, 4], "bfloat16"),
     "h0": ("psum", [128, 512], "float32"),
     "h1": ("psum", [128, 512], "float32"),
     "h2": ("psum", [128, 512], "float32"),
@@ -30,181 +32,239 @@ SCRATCH = {
     "ya": ("psum", [128, 512], "float32"),
     "yb": ("psum", [128, 512], "float32"),
 }
-SEMAPHORES = ["wl", "xl", "gl", "ml", "marr", "sent", "st", "fs", "tl", "hs", "rs", "gsd", "gq", "ms",
-              "yqa", "yqb", "ca", "cb"] + ["wa%d" % e for e in range(NX)]
+SEMAPHORES = (["wl", "xl", "gl", "ml", "marr", "sent", "st", "fs", "sd", "tl", "hs", "rs", "gsd", "gq", "ms",
+               "yqa", "yqb", "ca", "cb", "xarr", "garr", "gdl", "ada", "adb"]
+              + ["wa%d" % e for e in range(NX)] + ["p%d%d" % (q, a) for q in range(NH) for a in range(2)])
 
 
 def _bits(m):
     return [1 << b for b in range(16) if (m >> b) & 1]
 
 
-def _rows(route_r, kslots):
+def _join(bits):
+    m = 0
+    for b in bits:
+        m |= b
+    return m
+
+
+def _rows(route_r, kslots, experts):
     rows, span = [], {}
-    for e in range(NX):
+    for e in experts:
         sl = [i for i in range(kslots) if any(tok[i] == e for tok in route_r)]
-        if not sl:
-            continue
-        i0, i1 = min(sl), max(sl) + 1
+        i0, i1 = (min(sl), max(sl) + 1) if sl else (0, 1)
         span[e] = (len(rows), len(rows) + i1 - i0, i0, i1)
         for i in range(i0, i1):
             rows.append((e, i))
     return rows, span
 
 
-def _builder(g, core, T, topo, rank, which, nbuild):
-    route_r = T.tables["ROUTE"][rank]
-    rows, _ = _rows(route_r, T.tables["K"])
-    dst = T.cores[rank]
-    rid, pid, _se = topo.addr(dst)
-    eng = _bits(topo.mask(core, dst))
+def _group(T, topo, r):
+    cores = list(T.cores)
+    chips = sorted(set(topo.chip(c) for c in cores))
+    nch = len(chips)
+    me = chips.index(topo.chip(cores[r]))
+    mates = [s for s, c in enumerate(cores) if topo.chip(c) == chips[me] and s != r]
+    D, F = [], []
+    for k in range(1, nch):
+        for s, c in enumerate(cores):
+            if topo.chip(c) == chips[(me - k) % nch]:
+                (D if topo.die(c) == topo.die(cores[r]) else F).append(s)
+    team = [c for c in range(NSIM) if c not in cores
+            and topo.chip(c) == topo.chip(cores[r]) and topo.die(c) == topo.die(cores[r])]
+    workers = [cores[r]] + team[:NH]
+    assign = [[r] + mates + F[2:], [D[0], D[3]], [D[1], F[0]], [D[2], F[1]]]
+    return workers, assign, D, mates
+
+
+def _holder(T, topo, r, e):
+    workers, assign, _d, _m = _group(T, topo, r)
+    for w, lst in enumerate(assign):
+        if e in lst:
+            return workers[w]
+    raise ValueError("expert without a core")
+
+
+def _deal(T, r, assign):
+    route_r = T.tables["ROUTE"][r]
     pieces = []
-    for k, (e, i) in enumerate(rows):
-        for b in range(TOKS // BLK):
-            src = [j for j in range(BLK) if route_r[b * BLK + j][i] == e]
-            pieces.append((len(src), 4 * k + b, src))
-    pieces.sort(key=lambda p: (-p[0], p[1]))
-    mine = pieces[which::nbuild]
-    ne = len(eng)
-    calls = [mine[a:a + ne] for a in range(0, len(mine), ne)]
-    g.vector.memset(T.seed[:, 0:1], 1.0).then_inc(T.sem.fs, 1)
-    g.vector.memset(T.seed[:, 1:129], 0.0).then_inc(T.sem.fs, 1)
-    g.sync.wait_ge(T.sem.fs, 2)
-    g.sync.dma_start(T.eye[:], T.seed[:]).then_inc(T.sem.tl, 16)
-    g.wait_ge(T.sem.tl, 16)
-    total = 0
-    for ci, call in enumerate(calls):
-        if ci % 2:
-            call = call[::-1]
-        trs = []
-        for q, (_n, slot, src) in enumerate(call):
-            ids = list(src)
-            while len(ids) < 2:
-                ids.append(128)
-            if len(ids) > 64:
-                raise ValueError("a fold takes at most 64 sources")
-            trs.append(RemoteDMATransfer(dst_ids=[DstId(rid=rid, pnc=pid)], dma_engine_mask=eng[q],
-                                         remote_sem=T.sem.marr, srcs=[T.eye[j] for j in ids],
-                                         dsts=[T.mk[slot]], alu_op=1))
-            total += 1
-        g.remote_dma_fused(trs, local_sem=T.sem.sent)
-    g.wait_ge(T.sem.sent, total)
+    for w, lst in enumerate(assign):
+        rows, _ = _rows(route_r, T.tables["K"], lst)
+        for k, (e, i) in enumerate(rows):
+            for b in range(TOKS // BLK):
+                src = [j for j in range(BLK) if route_r[b * BLK + j][i] == e]
+                pieces.append((len(src), w, 4 * k + b, src))
+    pieces.sort(key=lambda p: (-p[0], p[1], p[2]))
+    cap = -(-len(pieces) // NH)
+    share = {q: [] for q in range(1, NH + 1)}
+    load = {q: 0 for q in range(1, NH + 1)}
+    for p in pieces:
+        ok = [q for q in share if q != p[1]]
+        room = [q for q in ok if len(share[q]) < cap] or ok
+        q = min(room, key=lambda z: (load[z], z))
+        share[q].append(p)
+        load[q] += max(p[0], 2)
+    for q in share:
+        while len(share[q]) > cap:
+            z = min(share, key=lambda u: len(share[u]))
+            p = [p for p in share[q] if p[1] != z][-1]
+            share[q].remove(p)
+            share[z].append(p)
+    for q in share:
+        share[q].sort(key=lambda p: (-p[0], p[1], p[2]))
+    return share
 
 
 def rank_program(g, core, T, topo):
     cores = list(T.cores)
-    rank = T.rank_of(core)
-    if rank is None:
-        for r, rc in enumerate(cores):
-            if topo.chip(rc) == topo.chip(core) and topo.die(rc) == topo.die(core):
-                team = [c for c in range(NSIM) if c not in cores
-                        and topo.chip(c) == topo.chip(rc) and topo.die(c) == topo.die(rc)]
-                _builder(g, core, T, topo, r, team.index(core), len(team))
-                return
-        return
-
     S = T.sem
-    route_r = T.tables["ROUTE"][rank]
-    rows, span = _rows(route_r, T.tables["K"])
-    KR = len(rows)
-
-    chips = sorted(set(topo.chip(c) for c in cores))
-    nch = len(chips)
-    me = chips.index(topo.chip(core))
-
-    def on_chip(ch):
-        return [r for r, c in enumerate(cores) if topo.chip(c) == ch]
-
-    def port_rank(ch, sender):
-        rs = on_chip(ch)
-        same = [r for r in rs if topo.die(cores[r]) == topo.die(cores[sender])]
-        return same[0] if same else rs[0]
-
-    mates = [r for r in on_chip(chips[me]) if r != rank]
-    out_peers = [port_rank(chips[(me + k) % nch], rank) for k in range(1, nch)]
-    direct, fwd = [], []
-    for k in range(1, nch):
-        for s in on_chip(chips[(me - k) % nch]):
-            (direct if port_rank(chips[me], s) == rank else fwd).append(s)
-    off_mask = topo.mask(core, cores[out_peers[0]])
-    on_mask = topo.mask(core, cores[mates[0]])
-    up = on_mask & ~off_mask
-    if len(_bits(up)) not in (1, 2, 4, 8, 16):
-        up = on_mask
-    n_off, n_on = len(_bits(off_mask)), len(_bits(up))
-    arrive = {}
-    for s in direct:
-        arrive[s] = n_off
-    for s in fwd + mates:
-        arrive[s] = n_on
-
-    order = [rank] + mates + direct[:3] + fwd[:1] + direct[3:4] + fwd[1:] + direct[4:]
-    order = [e for e in order if e in span]
+    r, w = None, None
+    for rr in range(len(cores)):
+        ws = _group(T, topo, rr)[0]
+        if core in ws:
+            r, w = rr, ws.index(core)
+    if r is None:
+        return
+    workers, assign, D, mates = _group(T, topo, r)
+    is_rank = (w == 0)
+    order = assign[w]
     NQ = len(order)
     last = NQ - 1
-    pre = min(PRE, NQ)
+    route_r = T.tables["ROUTE"][r]
+    rows, span = _rows(route_r, T.tables["K"], order)
+    KR = len(rows)
+    te, ve = g.tensor, g.vector
+
+    far = [c for c in cores if topo.chip(c) != topo.chip(core)][0]
+    near = [c for c in workers if c != core][0]
+    off_mask = topo.mask(core, far)
+    on_mask = topo.mask(core, near)
+    up = on_mask & ~off_mask
+    if len(_bits(up)) != 8:
+        up = _join(_bits(on_mask)[:8])
+    upb = _bits(up)
+    lowb = [b for b in _bits(on_mask) if b not in upb]
+    NE = 8
+    nsent = 0
 
     def wslot(e):
         return T.wall[:, 256 * e:256 * e + 256]
 
-    g.sync.dma_start(T.wall[:, 256 * rank:256 * rank + 128], T.w1[:, :]).then_inc(S.wl, 16)
-    g.scalar.dma_start(T.wall[:, 256 * rank + 128:256 * rank + 256], T.w2[:, :]).then_inc(S.wl, 16)
-    g.sync.dma_start(T.xs[:], T.x[:, :]).then_inc(S.xl, 16)
-    ngl = 0
-    for n, e in enumerate(sorted(span)):
-        k0, k1, i0, i1 = span[e]
-        q = g.scalar if n % 2 == 0 else g.sync
-        q.dma_start(T.grep[k0:k1, :], T.gate[i0:i1, :]).then_inc(S.gl, 16)
-        ngl += 16
-    g.sync.wait_ge(S.marr, 4 * KR)
-    g.sync.dma_start(T.mks[0:KR, :], T.mk[0:4 * KR]).then_inc(S.ml, 16)
-
-    nsent = 0
-
-    def send(e, dst_rank, mask):
-        rid, pid, _se = topo.addr(cores[dst_rank])
+    def send_w(e, dst, mask):
+        rid, pid, _se = topo.addr(dst)
         g.remote_dma(out_ap=wslot(e), in_ap=wslot(e), remote_sem=S["wa%d" % e], local_sem=S.sent,
                      pid=pid, routing_id=rid, dma_engine_mask=mask)
         return len(_bits(mask))
 
-    g.wait_ge(S.wl, 32)
-    nsent += send(rank, out_peers[0], off_mask)
-    for m in mates:
-        nsent += send(rank, m, up)
-    for p in out_peers[1:]:
-        nsent += send(rank, p, off_mask)
-    for s in direct:
-        g.wait_ge(S["wa%d" % s], arrive[s])
+    if is_rank:
+        g.sync.dma_start(T.wall[:, 256 * r:256 * r + 128], T.w1[:, :]).then_inc(S.wl, 16)
+        g.scalar.dma_start(T.wall[:, 256 * r + 128:256 * r + 256], T.w2[:, :]).then_inc(S.wl, 16)
+        g.sync.dma_start(T.xs[:], T.x[:, :]).then_inc(S.xl, 16)
+        g.scalar.dma_start(T.gd[:], T.gate[:, :]).then_inc(S.gdl, 16)
+        ngl = 0
+        for e in order:
+            k0, k1, i0, i1 = span[e]
+            g.scalar.dma_start(T.grep[k0:k1, :], T.gate[i0:i1, :]).then_inc(S.gl, 16)
+            ngl += 16
+        chips = sorted(set(topo.chip(c) for c in cores))
+        me = chips.index(topo.chip(core))
+        outs = []
+        for k in range(1, len(chips)):
+            peer = [s for s, c in enumerate(cores) if topo.chip(c) == chips[(me + k) % len(chips)]
+                    and topo.die(c) == topo.die(core)][0]
+            outs.append(_holder(T, topo, peer, r))
+        hid = [DstId(rid=topo.addr(c)[0], pnc=topo.addr(c)[1]) for c in workers[1:]]
+        g.wait_ge(S.wl, 32)
+        nsent += send_w(r, outs[0], off_mask)
+        g.wait_ge(S.xl, 16)
+        trs = []
+        for a in range(2):
+            ap = T.xs[:, 256 * a:256 * a + 256]
+            trs.append(RemoteDMATransfer(dst_ids=hid, dma_engine_mask=_join(upb[4 * a:4 * a + 4]),
+                                         remote_sem=S.xarr, srcs=[ap], dsts=[ap for _c in hid], alu_op=0))
+            nsent += 4
+        g.remote_dma_fused(trs, local_sem=S.sent)
+        g.wait_ge(S.gdl, 16)
+        trs = []
+        for i in range(3):
+            trs.append(RemoteDMATransfer(dst_ids=hid, dma_engine_mask=upb[i], remote_sem=S.garr,
+                                         srcs=[T.gd[i]], dsts=[T.gd[i] for _c in hid], alu_op=0))
+            nsent += 1
+        g.remote_dma_fused(trs, local_sem=S.sent)
+        nsent += send_w(r, outs[1], off_mask)
         for m in mates:
-            nsent += send(s, m, up)
+            nsent += send_w(r, _holder(T, topo, m, r), up)
+        for o in outs[2:]:
+            nsent += send_w(r, o, off_mask)
+    else:
+        ve.memset(T.seed[:, 0:1], 1.0).then_inc(S.sd, 1)
+        ve.memset(T.seed[:, 1:129], 0.0).then_inc(S.sd, 1)
+        g.sync.wait_ge(S.sd, 2)
+        g.sync.dma_start(T.eye[:], T.seed[:]).then_inc(S.tl, 16)
+        g.scalar.wait_ge(S.garr, 3)
+        ngl = 0
+        for e in order:
+            k0, k1, i0, i1 = span[e]
+            g.scalar.dma_start(T.grep[k0:k1, :], T.gd[i0:i1]).then_inc(S.gl, 16)
+            ngl += 16
+        mine = _deal(T, r, assign)[w]
+        eng = _bits(on_mask)
+        g.wait_ge(S.tl, 16)
+        for ci, a0 in enumerate(range(0, len(mine), len(eng))):
+            call = mine[a0:a0 + len(eng)]
+            if ci % 2:
+                call = call[::-1]
+            trs = []
+            for q, (_n, uw, slot, src) in enumerate(call):
+                ids = list(src)
+                while len(ids) < 2:
+                    ids.append(128)
+                if len(ids) > 64:
+                    raise ValueError("a fold takes at most 64 sources")
+                rid, pid, _se = topo.addr(workers[uw])
+                trs.append(RemoteDMATransfer(dst_ids=[DstId(rid=rid, pnc=pid)], dma_engine_mask=eng[q],
+                                             remote_sem=S.marr, srcs=[T.eye[j] for j in ids],
+                                             dsts=[T.mk[slot]], alu_op=1))
+                nsent += 1
+            g.remote_dma_fused(trs, local_sem=S.sent)
+        for e in order:
+            if e in D:
+                g.wait_ge(S["wa%d" % e], NE)
+                for m in mates:
+                    nsent += send_w(e, _holder(T, topo, m, e), up)
+    g.sync.wait_ge(S.marr, 4 * KR)
+    g.sync.dma_start(T.mks[0:KR, :], T.mk[0:4 * KR]).then_inc(S.ml, 16)
 
     H = [T.h0, T.h1, T.h2]
     GB = [T.g0, T.g1, T.g2]
     YP = [T.ya, T.yb]
     YQ = [S.yqa, S.yqb]
-    nfill = 2 + len(span) + len([e for e in span if span[e][0] > 0])
-    te, ve = g.tensor, g.vector
+    CS = [S.ca, S.cb]
+    nfill = 2 + NQ + len([e for e in order if span[e][0] > 0])
 
     def mm_h(n):
         e = order[n]
-        if e == rank:
+        if e == r and is_rank:
             te.wait_ge(S.wl, 32)
         else:
-            te.wait_ge(S["wa%d" % e], arrive[e])
+            te.wait_ge(S["wa%d" % e], NE)
         if n == 0:
-            te.wait_ge(S.xl, 16)
+            if is_rank:
+                te.wait_ge(S.xl, 16)
+            else:
+                te.wait_ge(S.xarr, 8)
         if n >= 3:
             te.wait_ge(S.rs, n - 2)
         te.matmul(out=H[n % 3][:], lhsT=T.wall[:, 256 * e:256 * e + 128], rhs=T.xs[:],
                   start=True, stop=True).then_inc(S.hs, 1)
 
     def mm_g(n):
-        e = order[n]
         if n == 0:
             te.wait_ge(S.fs, nfill)
             te.wait_ge(S.gsd, 1)
         if n >= 3:
             te.wait_ge(S.ms, 2 * (n - 2))
-        te.matmul(out=GB[n % 3][:], lhsT=T.sel[0:KR, 128 * e:128 * e + 128], rhs=T.gs[0:KR, :],
+        te.matmul(out=GB[n % 3][:], lhsT=T.sel[0:KR, 128 * n:128 * n + 128], rhs=T.gs[0:KR, :],
                   start=True, stop=True).then_inc(S.gq, 1)
 
     def mm_y(n):
@@ -215,29 +275,27 @@ def rank_program(g, core, T, topo):
                       rhs=T.rg[:, 512 * n + 256 * a:512 * n + 256 * a + 256],
                       start=(n == 0), stop=(n == last)).then_inc(YQ[a], 1)
 
-    for n in range(pre):
-        mm_h(n)
-    for n in range(min(3, NQ)):
-        mm_g(n)
-    for n in range(NQ):
-        if pre + n < NQ:
-            mm_h(pre + n)
-        mm_y(n)
-        if n + 3 < NQ:
-            mm_g(n + 3)
+    if is_rank:
+        pseq = [("h", 0), ("h", 1), ("g", 0), ("g", 1), ("g", 2), ("y", 0), ("g", 3), ("y", 1),
+                ("h", 2), ("h", 3), ("y", 2), ("y", 3)]
+        vseq = [("r", 0), ("r", 1), ("s", 0), ("m", 0), ("m", 1), ("r", 2), ("m", 2), ("r", 3), ("m", 3)]
+    else:
+        pseq = [("h", 0), ("g", 0), ("g", 1), ("h", 1), ("y", 0), ("y", 1)]
+        vseq = [("r", 0), ("s", 0), ("r", 1), ("m", 0), ("m", 1)]
+    for op, n in pseq:
+        (mm_h if op == "h" else mm_g if op == "g" else mm_y)(n)
 
     ve.memset(T.zeros[:], 0.0).then_inc(S.fs, 1)
     ve.memset(T.sel[0:KR, :], 0.0).then_inc(S.fs, 1)
     ve.wait_ge(S.fs, 2)
     nf = 2
-    for e in sorted(span):
-        ve.memset(T.sel[0:span[e][1], 128 * e:128 * e + 128], 1.0).then_inc(S.fs, 1)
+    for n, e in enumerate(order):
+        ve.memset(T.sel[0:span[e][1], 128 * n:128 * n + 128], 1.0).then_inc(S.fs, 1)
         nf += 1
     ve.wait_ge(S.fs, nf)
-    for e in sorted(span):
+    for n, e in enumerate(order):
         if span[e][0] > 0:
-            ve.memset(T.sel[0:span[e][0], 128 * e:128 * e + 128], 0.0).then_inc(S.fs, 1)
-            nf += 1
+            ve.memset(T.sel[0:span[e][0], 128 * n:128 * n + 128], 0.0).then_inc(S.fs, 1)
 
     def relu(n):
         ve.wait_ge(S.hs, n + 1)
@@ -256,27 +314,47 @@ def rank_program(g, core, T, topo):
                 ve.tensor_tensor(out=T.rg[:, c:c + 256], in0=T.r[:, c:c + 256],
                                  in1=GB[n % 3][:, 256 * a:256 * a + 256], op=AluOpType.mult).then_inc(S.ms, 1)
 
-    for n in range(pre):
-        relu(n)
-    ve.wait_ge(S.gl, ngl)
-    ve.wait_ge(S.ml, 16)
-    ve.tensor_tensor(out=T.gs[0:KR, :], in0=T.mks[0:KR, :], in1=T.grep[0:KR, :],
-                     op=AluOpType.mult).then_inc(S.gsd, 1)
-    for n in range(NQ):
-        if pre + n < NQ:
-            relu(pre + n)
-        gatemul(n)
-    CS = [S.ca, S.cb]
-    for a in range(2):
-        ve.wait_ge(YQ[a], NQ)
-        ve.tensor_copy(out=T.ysb[:, 256 * a:256 * a + 256], in_=YP[a][:, 0:256]).then_inc(CS[a], 1)
+    def gsmul(_n):
+        ve.wait_ge(S.gl, ngl)
+        ve.wait_ge(S.ml, 16)
+        ve.tensor_tensor(out=T.gs[0:KR, :], in0=T.mks[0:KR, :], in1=T.grep[0:KR, :],
+                         op=AluOpType.mult).then_inc(S.gsd, 1)
 
+    for op, n in vseq:
+        (relu if op == "r" else gsmul if op == "s" else gatemul)(n)
+
+    if not is_rank:
+        rid, pid, _se = topo.addr(workers[0])
+        for a in range(2):
+            ve.wait_ge(YQ[a], NQ)
+            ve.tensor_copy(out=T.ysb[:, 256 * a:256 * a + 256], in_=YP[a][:, 0:256]).then_inc(CS[a], 1)
+        for a in range(2):
+            c = 512 * (w - 1) + 256 * a
+            g.wait_ge(CS[a], 1)
+            g.remote_dma(out_ap=T.part[:, c:c + 256], in_ap=T.ysb[:, 256 * a:256 * a + 256],
+                         remote_sem=S["p%d%d" % (w - 1, a)], local_sem=S.sent, pid=pid, routing_id=rid,
+                         dma_engine_mask=_join(lowb if a == 0 else upb))
+            nsent += 8
+        g.wait_ge(S.sent, nsent)
+        return
+
+    AD = [S.ada, S.adb]
+    for q in range(NH):
+        for a in range(2):
+            if q == 0:
+                ve.wait_ge(YQ[a], NQ)
+            else:
+                ve.wait_ge(AD[a], q)
+            ve.wait_ge(S["p%d%d" % (q, a)], 8)
+            c = 512 * q + 256 * a
+            if q < NH - 1:
+                ve.tensor_tensor(out=YP[a][:, 0:256], in0=YP[a][:, 0:256], in1=T.part[:, c:c + 256],
+                                 op=AluOpType.add).then_inc(AD[a], 1)
+            else:
+                ve.tensor_tensor(out=T.ysb[:, 256 * a:256 * a + 256], in0=YP[a][:, 0:256],
+                                 in1=T.part[:, c:c + 256], op=AluOpType.add).then_inc(CS[a], 1)
     for a, q in enumerate((g.sync, g.scalar)):
         q.wait_ge(CS[a], 1)
         q.dma_start(T.y[:, 256 * a:256 * a + 256], T.ysb[:, 256 * a:256 * a + 256]).then_inc(S.st, 16)
-
     g.wait_ge(S.sent, nsent)
-    for e in range(NX):
-        if e != rank:
-            g.wait_ge(S["wa%d" % e], arrive[e])
     g.wait_ge(S.st, 32)

@@ -1,5 +1,5 @@
 from concourse.bass import DstId, RemoteDMATransfer
-from concourse.mybir import AluOpType
+from concourse.mybir import AluOpType, ActivationFunctionType
 
 NSIM = 80
 NX = 10
@@ -10,16 +10,18 @@ NH = 3
 SCRATCH = {
     "wall": ("sbuf", [128, NX * 256], "bfloat16"),
     "xs": ("sbuf", [128, TOKS], "bfloat16"),
-    "zeros": ("sbuf", [128, TOKS], "bfloat16"),
     "r": ("sbuf", [128, 4 * TOKS], "bfloat16"),
     "rg": ("sbuf", [128, 4 * TOKS], "bfloat16"),
-    "grep": ("sbuf", [128, TOKS], "bfloat16"),
+    "g3": ("sbuf", [128, TOKS], "bfloat16"),
+    "selg": ("sbuf", [128, 16], "bfloat16"),
     "mks": ("sbuf", [128, TOKS], "bfloat16"),
     "gs": ("sbuf", [128, TOKS], "bfloat16"),
     "sel": ("sbuf", [128, 4 * 128], "bfloat16"),
     "ysb": ("sbuf", [128, TOKS], "bfloat16"),
     "part": ("sbuf", [128, NH * TOKS], "bfloat16"),
     "seed": ("sbuf", [128, 129], "bfloat16"),
+    "ones": ("sbuf", [128, 128], "bfloat16"),
+    "ident": ("sbuf", [128, 128], "bfloat16"),
     "eye": ("dram", [129, 128, 1], "bfloat16"),
     "mk": ("dram", [3 * 4 * 4, 128, 1], "bfloat16"),
     "gd": ("dram", [3, 128, 4], "bfloat16"),
@@ -33,7 +35,7 @@ SCRATCH = {
     "yb": ("psum", [128, 512], "float32"),
 }
 SEMAPHORES = (["wl", "xl", "gl", "ml", "marr", "sent", "st", "fs", "sd", "tl", "hs", "rs", "gsd", "gq", "ms",
-               "yqa", "yqb", "ca", "cb", "xarr", "garr", "gdl", "ada", "adb"]
+               "yqa", "yqb", "ca", "cb", "xarr", "garr", "gdl", "ada", "gp", "on", "idn"]
               + ["wa%d" % e for e in range(NX)] + ["p%d%d" % (q, a) for q in range(NH) for a in range(2)])
 
 
@@ -85,7 +87,30 @@ def _holder(T, topo, r, e):
     raise ValueError("expert without a core")
 
 
-def _deal(T, r, assign):
+def _size(p):
+    return (-p[0], p[1], p[2])
+
+
+def _spread(pieces, base, cap):
+    pieces = sorted(pieces, key=_size)
+    share = {q: [] for q in range(1, NH + 1)}
+    load = {q: 0 for q in range(1, NH + 1)}
+    for p in pieces:
+        ok = [q for q in share if q != p[1]]
+        room = [q for q in ok if len(share[q]) + base[q] < cap] or ok
+        q = min(room, key=lambda z: (load[z], z))
+        share[q].append(p)
+        load[q] += max(p[0], 2)
+    for q in share:
+        while len(share[q]) + base[q] > cap:
+            z = min(share, key=lambda u: len(share[u]) + base[u])
+            p = [p for p in share[q] if p[1] != z][-1]
+            share[q].remove(p)
+            share[z].append(p)
+    return share
+
+
+def _deal(T, r, assign, neng):
     route_r = T.tables["ROUTE"][r]
     pieces = []
     for w, lst in enumerate(assign):
@@ -94,25 +119,21 @@ def _deal(T, r, assign):
             for b in range(TOKS // BLK):
                 src = [j for j in range(BLK) if route_r[b * BLK + j][i] == e]
                 pieces.append((len(src), w, 4 * k + b, src))
-    pieces.sort(key=lambda p: (-p[0], p[1], p[2]))
-    cap = -(-len(pieces) // NH)
-    share = {q: [] for q in range(1, NH + 1)}
-    load = {q: 0 for q in range(1, NH + 1)}
-    for p in pieces:
-        ok = [q for q in share if q != p[1]]
-        room = [q for q in ok if len(share[q]) < cap] or ok
-        q = min(room, key=lambda z: (load[z], z))
-        share[q].append(p)
-        load[q] += max(p[0], 2)
-    for q in share:
-        while len(share[q]) > cap:
-            z = min(share, key=lambda u: len(share[u]))
-            p = [p for p in share[q] if p[1] != z][-1]
-            share[q].remove(p)
-            share[z].append(p)
-    for q in share:
-        share[q].sort(key=lambda p: (-p[0], p[1], p[2]))
-    return share
+    p0 = [p for p in pieces if p[1] == 0]
+    p1 = [p for p in pieces if p[1] != 0]
+    first = _spread(p0, {q: 0 for q in range(1, NH + 1)}, -(-len(p0) // NH))
+    rest = _spread(p1, {q: len(first[q]) for q in first}, -(-len(pieces) // NH))
+    calls = {}
+    for q in first:
+        a = sorted(first[q], key=_size)
+        b = sorted(rest[q], key=_size)
+        calls[q] = [a[c:c + neng] for c in range(0, len(a), neng)]
+        nfil = min(len(b), neng - len(calls[q][-1])) if calls[q] else 0
+        if nfil:
+            calls[q][-1] = sorted(calls[q][-1] + b[len(b) - nfil:], key=_size)
+            b = b[:len(b) - nfil]
+        calls[q] += [b[c:c + neng] for c in range(0, len(b), neng)]
+    return calls
 
 
 def rank_program(g, core, T, topo):
@@ -130,10 +151,11 @@ def rank_program(g, core, T, topo):
     order = assign[w]
     NQ = len(order)
     last = NQ - 1
+    KS = T.tables["K"]
     route_r = T.tables["ROUTE"][r]
-    rows, span = _rows(route_r, T.tables["K"], order)
+    rows, span = _rows(route_r, KS, order)
     KR = len(rows)
-    te, ve = g.tensor, g.vector
+    te, ve, se = g.tensor, g.vector, g.scalar
 
     far = [c for c in cores if topo.chip(c) != topo.chip(core)][0]
     near = [c for c in workers if c != core][0]
@@ -158,14 +180,11 @@ def rank_program(g, core, T, topo):
 
     if is_rank:
         g.sync.dma_start(T.wall[:, 256 * r:256 * r + 128], T.w1[:, :]).then_inc(S.wl, 16)
-        g.scalar.dma_start(T.wall[:, 256 * r + 128:256 * r + 256], T.w2[:, :]).then_inc(S.wl, 16)
+        se.dma_start(T.wall[:, 256 * r + 128:256 * r + 256], T.w2[:, :]).then_inc(S.wl, 16)
+        se.dma_start(T.gd[:], T.gate[:, :]).then_inc(S.gdl, 16)
         g.sync.dma_start(T.xs[:], T.x[:, :]).then_inc(S.xl, 16)
-        g.scalar.dma_start(T.gd[:], T.gate[:, :]).then_inc(S.gdl, 16)
-        ngl = 0
-        for e in order:
-            k0, k1, i0, i1 = span[e]
-            g.scalar.dma_start(T.grep[k0:k1, :], T.gate[i0:i1, :]).then_inc(S.gl, 16)
-            ngl += 16
+        se.dma_start(T.g3[0:KS, :], T.gate[:, :]).then_inc(S.gl, 16)
+        ve.memset(T.ones[:], 1.0).then_inc(S.on, 1)
         chips = sorted(set(topo.chip(c) for c in cores))
         me = chips.index(topo.chip(core))
         outs = []
@@ -176,42 +195,36 @@ def rank_program(g, core, T, topo):
         hid = [DstId(rid=topo.addr(c)[0], pnc=topo.addr(c)[1]) for c in workers[1:]]
         g.wait_ge(S.wl, 32)
         nsent += send_w(r, outs[0], off_mask)
-        g.wait_ge(S.xl, 16)
-        trs = []
-        for a in range(2):
-            ap = T.xs[:, 256 * a:256 * a + 256]
-            trs.append(RemoteDMATransfer(dst_ids=hid, dma_engine_mask=_join(upb[4 * a:4 * a + 4]),
-                                         remote_sem=S.xarr, srcs=[ap], dsts=[ap for _c in hid], alu_op=0))
-            nsent += 4
-        g.remote_dma_fused(trs, local_sem=S.sent)
+        nsent += send_w(r, outs[1], off_mask)
         g.wait_ge(S.gdl, 16)
         trs = []
-        for i in range(3):
+        for i in range(KS):
             trs.append(RemoteDMATransfer(dst_ids=hid, dma_engine_mask=upb[i], remote_sem=S.garr,
                                          srcs=[T.gd[i]], dsts=[T.gd[i] for _c in hid], alu_op=0))
             nsent += 1
         g.remote_dma_fused(trs, local_sem=S.sent)
-        nsent += send_w(r, outs[1], off_mask)
+        g.wait_ge(S.xl, 16)
+        g.remote_dma_fused([RemoteDMATransfer(dst_ids=hid, dma_engine_mask=up, remote_sem=S.xarr,
+                                              srcs=[T.xs[:]], dsts=[T.xs[:] for _c in hid], alu_op=0)],
+                           local_sem=S.sent)
+        nsent += len(upb)
         for m in mates:
             nsent += send_w(r, _holder(T, topo, m, r), up)
         for o in outs[2:]:
             nsent += send_w(r, o, off_mask)
+        g.wait_ge(S.on, 1)
+        g.affine_select(T.ident[:], T.ones[:], [[-1, 128]], AluOpType.is_equal, 0.0, 0, 1).then_inc(S.idn, 1)
     else:
         ve.memset(T.seed[:, 0:1], 1.0).then_inc(S.sd, 1)
         ve.memset(T.seed[:, 1:129], 0.0).then_inc(S.sd, 1)
         g.sync.wait_ge(S.sd, 2)
         g.sync.dma_start(T.eye[:], T.seed[:]).then_inc(S.tl, 16)
-        g.scalar.wait_ge(S.garr, 3)
-        ngl = 0
-        for e in order:
-            k0, k1, i0, i1 = span[e]
-            g.scalar.dma_start(T.grep[k0:k1, :], T.gd[i0:i1]).then_inc(S.gl, 16)
-            ngl += 16
-        mine = _deal(T, r, assign)[w]
+        g.sync.wait_ge(S.garr, KS)
+        g.sync.dma_start(T.g3[0:KS, :], T.gd[:]).then_inc(S.gl, 16)
         eng = _bits(on_mask)
+        mine = _deal(T, r, assign, len(eng))[w]
         g.wait_ge(S.tl, 16)
-        for ci, a0 in enumerate(range(0, len(mine), len(eng))):
-            call = mine[a0:a0 + len(eng)]
+        for ci, call in enumerate(mine):
             if ci % 2:
                 call = call[::-1]
             trs = []
@@ -238,9 +251,10 @@ def rank_program(g, core, T, topo):
     H = [T.h0, T.h1, T.h2]
     GB = [T.g0, T.g1, T.g2]
     YP = [T.ya, T.yb]
+    HL = [T.h0, T.h1] if is_rank else [T.h1, T.h2]
     YQ = [S.yqa, S.yqb]
     CS = [S.ca, S.cb]
-    nfill = 2 + NQ + len([e for e in order if span[e][0] > 0])
+    nfill = (2 + NQ + KR + len([e for e in order if span[e][0] > 0]) + len([k for k in rows if k[1] > 0]))
 
     def mm_h(n):
         e = order[n]
@@ -253,14 +267,24 @@ def rank_program(g, core, T, topo):
                 te.wait_ge(S.xl, 16)
             else:
                 te.wait_ge(S.xarr, 8)
-        if n >= 3:
-            te.wait_ge(S.rs, n - 2)
+        if n == last:
+            if is_rank:
+                te.wait_ge(S.rs, 2)
+            for a in range(2):
+                te.matmul(out=HL[a][:, 0:256], lhsT=T.wall[:, 256 * e:256 * e + 128],
+                          rhs=T.xs[:, 256 * a:256 * a + 256], start=True, stop=True).then_inc(S.hs, 1)
+            return
         te.matmul(out=H[n % 3][:], lhsT=T.wall[:, 256 * e:256 * e + 128], rhs=T.xs[:],
                   start=True, stop=True).then_inc(S.hs, 1)
 
+    def mm_p(_n):
+        te.wait_ge(S.fs, nfill)
+        te.wait_ge(S.gl, 16)
+        te.matmul(out=T.g2[0:KR, :], lhsT=T.selg[0:KS, 0:KR], rhs=T.g3[0:KS, :],
+                  start=True, stop=True).then_inc(S.gp, 1)
+
     def mm_g(n):
         if n == 0:
-            te.wait_ge(S.fs, nfill)
             te.wait_ge(S.gsd, 1)
         if n >= 3:
             te.wait_ge(S.ms, 2 * (n - 2))
@@ -273,36 +297,57 @@ def rank_program(g, core, T, topo):
             te.wait_ge(S.ms, 2 * n + 2 if n < last else 2 * n + 1 + a)
             te.matmul(out=YP[a][:, 0:256], lhsT=T.wall[:, 256 * e + 128:256 * e + 256],
                       rhs=T.rg[:, 512 * n + 256 * a:512 * n + 256 * a + 256],
-                      start=(n == 0), stop=(n == last)).then_inc(YQ[a], 1)
+                      start=(n == 0), stop=(n == last and not (is_rank and a == 1))).then_inc(YQ[a], 1)
 
     if is_rank:
-        pseq = [("h", 0), ("h", 1), ("g", 0), ("g", 1), ("g", 2), ("y", 0), ("g", 3), ("y", 1),
-                ("h", 2), ("h", 3), ("y", 2), ("y", 3)]
-        vseq = [("r", 0), ("r", 1), ("s", 0), ("m", 0), ("m", 1), ("r", 2), ("m", 2), ("r", 3), ("m", 3)]
+        pseq = [("h", 0), ("p", 0), ("h", 1), ("g", 0), ("g", 1), ("g", 2), ("y", 0), ("h", 2), ("g", 3),
+                ("y", 1), ("h", 3), ("y", 2), ("y", 3)]
     else:
-        pseq = [("h", 0), ("g", 0), ("g", 1), ("h", 1), ("y", 0), ("y", 1)]
-        vseq = [("r", 0), ("s", 0), ("r", 1), ("m", 0), ("m", 1)]
+        pseq = [("p", 0), ("h", 0), ("g", 0), ("g", 1), ("h", 1), ("y", 0), ("y", 1)]
     for op, n in pseq:
-        (mm_h if op == "h" else mm_g if op == "g" else mm_y)(n)
+        (mm_h if op == "h" else mm_g if op == "g" else mm_p if op == "p" else mm_y)(n)
+    qord = sorted(range(NH), key=lambda q: (D[-1] in assign[q + 1], q))
+    if is_rank:
+        te.wait_ge(S.idn, 1)
+        for q in qord[:-1]:
+            te.wait_ge(S["p%d1" % q], 8)
+            c = 512 * q + 256
+            te.matmul(out=YP[1][:, 0:256], lhsT=T.ident[:], rhs=T.part[:, c:c + 256],
+                      start=False, stop=(q == qord[-2])).then_inc(YQ[1], 1)
 
-    ve.memset(T.zeros[:], 0.0).then_inc(S.fs, 1)
+    for n in range(NQ):
+        if n == last:
+            for a in range(2):
+                c = 512 * n + 256 * a
+                se.wait_ge(S.hs, n + 1 + a)
+                se.activation(T.r[:, c:c + 256], HL[a][:, 0:256], ActivationFunctionType.Relu).then_inc(S.rs, 1)
+            continue
+        se.wait_ge(S.hs, n + 1)
+        se.activation(T.r[:, 512 * n:512 * n + 512], H[n % 3][:], ActivationFunctionType.Relu).then_inc(S.rs, 1)
+
     ve.memset(T.sel[0:KR, :], 0.0).then_inc(S.fs, 1)
+    ve.memset(T.selg[0:KS, :], 0.0).then_inc(S.fs, 1)
     ve.wait_ge(S.fs, 2)
     nf = 2
     for n, e in enumerate(order):
         ve.memset(T.sel[0:span[e][1], 128 * n:128 * n + 128], 1.0).then_inc(S.fs, 1)
         nf += 1
+    for k, (_e, i) in enumerate(rows):
+        ve.memset(T.selg[0:i + 1, k:k + 1], 1.0).then_inc(S.fs, 1)
+        nf += 1
     ve.wait_ge(S.fs, nf)
     for n, e in enumerate(order):
         if span[e][0] > 0:
             ve.memset(T.sel[0:span[e][0], 128 * n:128 * n + 128], 0.0).then_inc(S.fs, 1)
+    for k, (_e, i) in enumerate(rows):
+        if i > 0:
+            ve.memset(T.selg[0:i, k:k + 1], 0.0).then_inc(S.fs, 1)
 
-    def relu(n):
-        ve.wait_ge(S.hs, n + 1)
-        ve.tensor_tensor(out=T.r[:, 512 * n:512 * n + 512], in0=H[n % 3][:], in1=T.zeros[:],
-                         op=AluOpType.max).then_inc(S.rs, 1)
-
-    def gatemul(n):
+    ve.wait_ge(S.gp, 1)
+    ve.wait_ge(S.ml, 16)
+    ve.tensor_tensor(out=T.gs[0:KR, :], in0=T.mks[0:KR, :], in1=T.g2[0:KR, :],
+                     op=AluOpType.mult).then_inc(S.gsd, 1)
+    for n in range(NQ):
         ve.wait_ge(S.gq, n + 1)
         ve.wait_ge(S.rs, n + 1)
         if n < last:
@@ -311,23 +356,16 @@ def rank_program(g, core, T, topo):
         else:
             for a in range(2):
                 c = 512 * n + 256 * a
+                ve.wait_ge(S.rs, n + 1 + a)
                 ve.tensor_tensor(out=T.rg[:, c:c + 256], in0=T.r[:, c:c + 256],
                                  in1=GB[n % 3][:, 256 * a:256 * a + 256], op=AluOpType.mult).then_inc(S.ms, 1)
 
-    def gsmul(_n):
-        ve.wait_ge(S.gl, ngl)
-        ve.wait_ge(S.ml, 16)
-        ve.tensor_tensor(out=T.gs[0:KR, :], in0=T.mks[0:KR, :], in1=T.grep[0:KR, :],
-                         op=AluOpType.mult).then_inc(S.gsd, 1)
-
-    for op, n in vseq:
-        (relu if op == "r" else gsmul if op == "s" else gatemul)(n)
-
     if not is_rank:
         rid, pid, _se = topo.addr(workers[0])
-        for a in range(2):
-            ve.wait_ge(YQ[a], NQ)
-            ve.tensor_copy(out=T.ysb[:, 256 * a:256 * a + 256], in_=YP[a][:, 0:256]).then_inc(CS[a], 1)
+        ve.wait_ge(YQ[0], NQ)
+        ve.tensor_copy(out=T.ysb[:, 0:256], in_=YP[0][:, 0:256]).then_inc(CS[0], 1)
+        se.wait_ge(YQ[1], NQ)
+        se.activation(T.ysb[:, 256:512], YP[1][:, 0:256], ActivationFunctionType.Copy).then_inc(CS[1], 1)
         for a in range(2):
             c = 512 * (w - 1) + 256 * a
             g.wait_ge(CS[a], 1)
@@ -338,22 +376,25 @@ def rank_program(g, core, T, topo):
         g.wait_ge(S.sent, nsent)
         return
 
-    AD = [S.ada, S.adb]
-    for q in range(NH):
-        for a in range(2):
-            if q == 0:
-                ve.wait_ge(YQ[a], NQ)
-            else:
-                ve.wait_ge(AD[a], q)
-            ve.wait_ge(S["p%d%d" % (q, a)], 8)
-            c = 512 * q + 256 * a
-            if q < NH - 1:
-                ve.tensor_tensor(out=YP[a][:, 0:256], in0=YP[a][:, 0:256], in1=T.part[:, c:c + 256],
-                                 op=AluOpType.add).then_inc(AD[a], 1)
-            else:
-                ve.tensor_tensor(out=T.ysb[:, 256 * a:256 * a + 256], in0=YP[a][:, 0:256],
-                                 in1=T.part[:, c:c + 256], op=AluOpType.add).then_inc(CS[a], 1)
-    for a, q in enumerate((g.sync, g.scalar)):
+    for j, q in enumerate(qord):
+        if j == 0:
+            ve.wait_ge(YQ[0], NQ)
+        else:
+            ve.wait_ge(S.ada, j)
+        ve.wait_ge(S["p%d0" % q], 8)
+        c = 512 * q
+        if j < NH - 1:
+            ve.tensor_tensor(out=YP[0][:, 0:256], in0=YP[0][:, 0:256], in1=T.part[:, c:c + 256],
+                             op=AluOpType.add).then_inc(S.ada, 1)
+        else:
+            ve.tensor_tensor(out=T.ysb[:, 0:256], in0=YP[0][:, 0:256], in1=T.part[:, c:c + 256],
+                             op=AluOpType.add).then_inc(CS[0], 1)
+    c = 512 * qord[-1] + 256
+    ve.wait_ge(YQ[1], NQ + NH - 1)
+    ve.wait_ge(S["p%d1" % qord[-1]], 8)
+    ve.tensor_tensor(out=T.ysb[:, 256:512], in0=YP[1][:, 0:256], in1=T.part[:, c:c + 256],
+                     op=AluOpType.add).then_inc(CS[1], 1)
+    for a, q in enumerate((g.sync, se)):
         q.wait_ge(CS[a], 1)
         q.dma_start(T.y[:, 256 * a:256 * a + 256], T.ysb[:, 256 * a:256 * a + 256]).then_inc(S.st, 16)
     g.wait_ge(S.sent, nsent)

from concourse.bass import DstId, RemoteDMATransfer
from concourse.mybir import AluOpType, ActivationFunctionType

NSIM = 80
NX = 10
TOKS = 512
BLK = 128
NH = 3

SCRATCH = {
    "wall": ("sbuf", [128, NX * 256], "bfloat16"),
    "xs": ("sbuf", [128, TOKS], "bfloat16"),
    "r": ("sbuf", [128, 4 * TOKS], "bfloat16"),
    "rg": ("sbuf", [128, 4 * TOKS], "bfloat16"),
    "g3": ("sbuf", [128, TOKS], "bfloat16"),
    "selg": ("sbuf", [128, 16], "bfloat16"),
    "mks": ("sbuf", [128, TOKS], "bfloat16"),
    "gs": ("sbuf", [128, TOKS], "bfloat16"),
    "sel": ("sbuf", [128, 4 * 128], "bfloat16"),
    "ysb": ("sbuf", [128, TOKS], "bfloat16"),
    "part": ("sbuf", [128, NH * TOKS], "bfloat16"),
    "seed": ("sbuf", [128, 129], "bfloat16"),
    "ones": ("sbuf", [128, 128], "bfloat16"),
    "ident": ("sbuf", [128, 128], "bfloat16"),
    "eye": ("dram", [129, 128, 1], "bfloat16"),
    "mk": ("dram", [3 * 4 * 4, 128, 1], "bfloat16"),
    "gd": ("dram", [3, 128, 4], "bfloat16"),
    "h0": ("psum", [128, 512], "float32"),
    "h1": ("psum", [128, 512], "float32"),
    "h2": ("psum", [128, 512], "float32"),
    "g0": ("psum", [128, 512], "float32"),
    "g1": ("psum", [128, 512], "float32"),
    "g2": ("psum", [128, 512], "float32"),
    "ya": ("psum", [128, 512], "float32"),
    "yb": ("psum", [128, 512], "float32"),
}
SEMAPHORES = (["wl", "xl", "gl", "ml", "marr", "sent", "st", "fs", "sd", "tl", "hs", "rs", "gsd", "gq", "ms",
               "yqa", "yqb", "ca", "cb", "xarr", "garr", "gdl", "ada", "gp", "on", "idn"]
              + ["wa%d" % e for e in range(NX)] + ["p%d%d" % (q, a) for q in range(NH) for a in range(2)])


def _bits(m):
    return [1 << b for b in range(16) if (m >> b) & 1]


def _join(bits):
    m = 0
    for b in bits:
        m |= b
    return m


def _rows(route_r, kslots, experts):
    rows, span = [], {}
    for e in experts:
        sl = [i for i in range(kslots) if any(tok[i] == e for tok in route_r)]
        i0, i1 = (min(sl), max(sl) + 1) if sl else (0, 1)
        span[e] = (len(rows), len(rows) + i1 - i0, i0, i1)
        for i in range(i0, i1):
            rows.append((e, i))
    return rows, span


def _group(T, topo, r):
    cores = list(T.cores)
    chips = sorted(set(topo.chip(c) for c in cores))
    nch = len(chips)
    me = chips.index(topo.chip(cores[r]))
    mates = [s for s, c in enumerate(cores) if topo.chip(c) == chips[me] and s != r]
    D, F = [], []
    for k in range(1, nch):
        for s, c in enumerate(cores):
            if topo.chip(c) == chips[(me - k) % nch]:
                (D if topo.die(c) == topo.die(cores[r]) else F).append(s)
    team = [c for c in range(NSIM) if c not in cores
            and topo.chip(c) == topo.chip(cores[r]) and topo.die(c) == topo.die(cores[r])]
    workers = [cores[r]] + team[:NH]
    assign = [[r] + mates + F[2:], [D[0], D[3]], [D[1], F[0]], [D[2], F[1]]]
    return workers, assign, D, mates


def _holder(T, topo, r, e):
    workers, assign, _d, _m = _group(T, topo, r)
    for w, lst in enumerate(assign):
        if e in lst:
            return workers[w]
    raise ValueError("expert without a core")


def _size(p):
    return (-p[0], p[1], p[2])


def _spread(pieces, base, cap):
    pieces = sorted(pieces, key=_size)
    share = {q: [] for q in range(1, NH + 1)}
    load = {q: 0 for q in range(1, NH + 1)}
    for p in pieces:
        ok = [q for q in share if q != p[1]]
        room = [q for q in ok if len(share[q]) + base[q] < cap] or ok
        q = min(room, key=lambda z: (load[z], z))
        share[q].append(p)
        load[q] += max(p[0], 2)
    for q in share:
        while len(share[q]) + base[q] > cap:
            z = min(share, key=lambda u: len(share[u]) + base[u])
            p = [p for p in share[q] if p[1] != z][-1]
            share[q].remove(p)
            share[z].append(p)
    return share


def _deal(T, r, assign, neng):
    route_r = T.tables["ROUTE"][r]
    pieces = []
    for w, lst in enumerate(assign):
        rows, _ = _rows(route_r, T.tables["K"], lst)
        for k, (e, i) in enumerate(rows):
            for b in range(TOKS // BLK):
                src = [j for j in range(BLK) if route_r[b * BLK + j][i] == e]
                pieces.append((len(src), w, 4 * k + b, src))
    p0 = [p for p in pieces if p[1] == 0]
    p1 = [p for p in pieces if p[1] != 0]
    first = _spread(p0, {q: 0 for q in range(1, NH + 1)}, -(-len(p0) // NH))
    rest = _spread(p1, {q: len(first[q]) for q in first}, -(-len(pieces) // NH))
    calls = {}
    for q in first:
        a = sorted(first[q], key=_size)
        b = sorted(rest[q], key=_size)
        calls[q] = [a[c:c + neng] for c in range(0, len(a), neng)]
        nfil = min(len(b), neng - len(calls[q][-1])) if calls[q] else 0
        if nfil:
            calls[q][-1] = sorted(calls[q][-1] + b[len(b) - nfil:], key=_size)
            b = b[:len(b) - nfil]
        calls[q] += [b[c:c + neng] for c in range(0, len(b), neng)]
    return calls


def rank_program(g, core, T, topo):
    cores = list(T.cores)
    S = T.sem
    r, w = None, None
    for rr in range(len(cores)):
        ws = _group(T, topo, rr)[0]
        if core in ws:
            r, w = rr, ws.index(core)
    if r is None:
        return
    workers, assign, D, mates = _group(T, topo, r)
    is_rank = (w == 0)
    order = assign[w]
    NQ = len(order)
    last = NQ - 1
    KS = T.tables["K"]
    route_r = T.tables["ROUTE"][r]
    rows, span = _rows(route_r, KS, order)
    KR = len(rows)
    te, ve, se = g.tensor, g.vector, g.scalar

    far = [c for c in cores if topo.chip(c) != topo.chip(core)][0]
    near = [c for c in workers if c != core][0]
    off_mask = topo.mask(core, far)
    on_mask = topo.mask(core, near)
    up = on_mask & ~off_mask
    if len(_bits(up)) != 8:
        up = _join(_bits(on_mask)[:8])
    upb = _bits(up)
    lowb = [b for b in _bits(on_mask) if b not in upb]
    NE = 8
    nsent = 0

    def wslot(e):
        return T.wall[:, 256 * e:256 * e + 256]

    def send_w(e, dst, mask):
        rid, pid, _se = topo.addr(dst)
        g.remote_dma(out_ap=wslot(e), in_ap=wslot(e), remote_sem=S["wa%d" % e], local_sem=S.sent,
                     pid=pid, routing_id=rid, dma_engine_mask=mask)
        return len(_bits(mask))

    if is_rank:
        g.sync.dma_start(T.wall[:, 256 * r:256 * r + 128], T.w1[:, :]).then_inc(S.wl, 16)
        se.dma_start(T.wall[:, 256 * r + 128:256 * r + 256], T.w2[:, :]).then_inc(S.wl, 16)
        se.dma_start(T.gd[:], T.gate[:, :]).then_inc(S.gdl, 16)
        g.sync.dma_start(T.xs[:], T.x[:, :]).then_inc(S.xl, 16)
        se.dma_start(T.g3[0:KS, :], T.gate[:, :]).then_inc(S.gl, 16)
        ve.memset(T.ones[:], 1.0).then_inc(S.on, 1)
        chips = sorted(set(topo.chip(c) for c in cores))
        me = chips.index(topo.chip(core))
        outs = []
        for k in range(1, len(chips)):
            peer = [s for s, c in enumerate(cores) if topo.chip(c) == chips[(me + k) % len(chips)]
                    and topo.die(c) == topo.die(core)][0]
            outs.append(_holder(T, topo, peer, r))
        hid = [DstId(rid=topo.addr(c)[0], pnc=topo.addr(c)[1]) for c in workers[1:]]
        g.wait_ge(S.wl, 32)
        nsent += send_w(r, outs[0], off_mask)
        nsent += send_w(r, outs[1], off_mask)
        g.wait_ge(S.gdl, 16)
        trs = []
        for i in range(KS):
            trs.append(RemoteDMATransfer(dst_ids=hid, dma_engine_mask=upb[i], remote_sem=S.garr,
                                         srcs=[T.gd[i]], dsts=[T.gd[i] for _c in hid], alu_op=0))
            nsent += 1
        g.remote_dma_fused(trs, local_sem=S.sent)
        g.wait_ge(S.xl, 16)
        g.remote_dma_fused([RemoteDMATransfer(dst_ids=hid, dma_engine_mask=up, remote_sem=S.xarr,
                                              srcs=[T.xs[:]], dsts=[T.xs[:] for _c in hid], alu_op=0)],
                           local_sem=S.sent)
        nsent += len(upb)
        for m in mates:
            nsent += send_w(r, _holder(T, topo, m, r), up)
        for o in outs[2:]:
            nsent += send_w(r, o, off_mask)
        g.wait_ge(S.on, 1)
        g.affine_select(T.ident[:], T.ones[:], [[-1, 128]], AluOpType.is_equal, 0.0, 0, 1).then_inc(S.idn, 1)
    else:
        ve.memset(T.seed[:, 0:1], 1.0).then_inc(S.sd, 1)
        ve.memset(T.seed[:, 1:129], 0.0).then_inc(S.sd, 1)
        g.sync.wait_ge(S.sd, 2)
        g.sync.dma_start(T.eye[:], T.seed[:]).then_inc(S.tl, 16)
        g.sync.wait_ge(S.garr, KS)
        g.sync.dma_start(T.g3[0:KS, :], T.gd[:]).then_inc(S.gl, 16)
        eng = _bits(on_mask)
        mine = _deal(T, r, assign, len(eng))[w]
        g.wait_ge(S.tl, 16)
        for ci, call in enumerate(mine):
            if ci % 2:
                call = call[::-1]
            trs = []
            for q, (_n, uw, slot, src) in enumerate(call):
                ids = list(src)
                while len(ids) < 2:
                    ids.append(128)
                if len(ids) > 64:
                    raise ValueError("a fold takes at most 64 sources")
                rid, pid, _se = topo.addr(workers[uw])
                trs.append(RemoteDMATransfer(dst_ids=[DstId(rid=rid, pnc=pid)], dma_engine_mask=eng[q],
                                             remote_sem=S.marr, srcs=[T.eye[j] for j in ids],
                                             dsts=[T.mk[slot]], alu_op=1))
                nsent += 1
            g.remote_dma_fused(trs, local_sem=S.sent)
        for e in order:
            if e in D:
                g.wait_ge(S["wa%d" % e], NE)
                for m in mates:
                    nsent += send_w(e, _holder(T, topo, m, e), up)
    g.sync.wait_ge(S.marr, 4 * KR)
    g.sync.dma_start(T.mks[0:KR, :], T.mk[0:4 * KR]).then_inc(S.ml, 16)

    H = [T.h0, T.h1, T.h2]
    GB = [T.g0, T.g1, T.g2]
    YP = [T.ya, T.yb]
    HL = [T.h0, T.h1] if is_rank else [T.h1, T.h2]
    YQ = [S.yqa, S.yqb]
    CS = [S.ca, S.cb]
    nfill = (2 + NQ + KR + len([e for e in order if span[e][0] > 0]) + len([k for k in rows if k[1] > 0]))

    def mm_h(n):
        e = order[n]
        if e == r and is_rank:
            te.wait_ge(S.wl, 32)
        else:
            te.wait_ge(S["wa%d" % e], NE)
        if n == 0:
            if is_rank:
                te.wait_ge(S.xl, 16)
            else:
                te.wait_ge(S.xarr, 8)
        if n == last:
            if is_rank:
                te.wait_ge(S.rs, 2)
            for a in range(2):
                te.matmul(out=HL[a][:, 0:256], lhsT=T.wall[:, 256 * e:256 * e + 128],
                          rhs=T.xs[:, 256 * a:256 * a + 256], start=True, stop=True).then_inc(S.hs, 1)
            return
        te.matmul(out=H[n % 3][:], lhsT=T.wall[:, 256 * e:256 * e + 128], rhs=T.xs[:],
                  start=True, stop=True).then_inc(S.hs, 1)

    def mm_p(_n):
        te.wait_ge(S.fs, nfill)
        te.wait_ge(S.gl, 16)
        te.matmul(out=T.g2[0:KR, :], lhsT=T.selg[0:KS, 0:KR], rhs=T.g3[0:KS, :],
                  start=True, stop=True).then_inc(S.gp, 1)

    def mm_g(n):
        if n == 0:
            te.wait_ge(S.gsd, 1)
        if n >= 3:
            te.wait_ge(S.ms, 2 * (n - 2))
        te.matmul(out=GB[n % 3][:], lhsT=T.sel[0:KR, 128 * n:128 * n + 128], rhs=T.gs[0:KR, :],
                  start=True, stop=True).then_inc(S.gq, 1)

    def mm_y(n):
        e = order[n]
        for a in range(2):
            te.wait_ge(S.ms, 2 * n + 2 if n < last else 2 * n + 1 + a)
            te.matmul(out=YP[a][:, 0:256], lhsT=T.wall[:, 256 * e + 128:256 * e + 256],
                      rhs=T.rg[:, 512 * n + 256 * a:512 * n + 256 * a + 256],
                      start=(n == 0), stop=(n == last and not (is_rank and a == 1))).then_inc(YQ[a], 1)

    if is_rank:
        pseq = [("h", 0), ("p", 0), ("h", 1), ("g", 0), ("g", 1), ("g", 2), ("y", 0), ("h", 2), ("g", 3),
                ("y", 1), ("h", 3), ("y", 2), ("y", 3)]
    else:
        pseq = [("p", 0), ("h", 0), ("g", 0), ("g", 1), ("h", 1), ("y", 0), ("y", 1)]
    for op, n in pseq:
        (mm_h if op == "h" else mm_g if op == "g" else mm_p if op == "p" else mm_y)(n)
    qord = sorted(range(NH), key=lambda q: (D[-1] in assign[q + 1], q))
    if is_rank:
        te.wait_ge(S.idn, 1)
        for q in qord[:-1]:
            te.wait_ge(S["p%d1" % q], 8)
            c = 512 * q + 256
            te.matmul(out=YP[1][:, 0:256], lhsT=T.ident[:], rhs=T.part[:, c:c + 256],
                      start=False, stop=(q == qord[-2])).then_inc(YQ[1], 1)

    for n in range(NQ):
        if n == last:
            for a in range(2):
                c = 512 * n + 256 * a
                se.wait_ge(S.hs, n + 1 + a)
                se.activation(T.r[:, c:c + 256], HL[a][:, 0:256], ActivationFunctionType.Relu).then_inc(S.rs, 1)
            continue
        se.wait_ge(S.hs, n + 1)
        se.activation(T.r[:, 512 * n:512 * n + 512], H[n % 3][:], ActivationFunctionType.Relu).then_inc(S.rs, 1)

    ve.memset(T.sel[0:KR, :], 0.0).then_inc(S.fs, 1)
    ve.memset(T.selg[0:KS, :], 0.0).then_inc(S.fs, 1)
    ve.wait_ge(S.fs, 2)
    nf = 2
    for n, e in enumerate(order):
        ve.memset(T.sel[0:span[e][1], 128 * n:128 * n + 128], 1.0).then_inc(S.fs, 1)
        nf += 1
    for k, (_e, i) in enumerate(rows):
        ve.memset(T.selg[0:i + 1, k:k + 1], 1.0).then_inc(S.fs, 1)
        nf += 1
    ve.wait_ge(S.fs, nf)
    for n, e in enumerate(order):
        if span[e][0] > 0:
            ve.memset(T.sel[0:span[e][0], 128 * n:128 * n + 128], 0.0).then_inc(S.fs, 1)
    for k, (_e, i) in enumerate(rows):
        if i > 0:
            ve.memset(T.selg[0:i, k:k + 1], 0.0).then_inc(S.fs, 1)

    ve.wait_ge(S.gp, 1)
    ve.wait_ge(S.ml, 16)
    ve.tensor_tensor(out=T.gs[0:KR, :], in0=T.mks[0:KR, :], in1=T.g2[0:KR, :],
                     op=AluOpType.mult).then_inc(S.gsd, 1)
    for n in range(NQ):
        ve.wait_ge(S.gq, n + 1)
        ve.wait_ge(S.rs, n + 1)
        if n < last:
            ve.tensor_tensor(out=T.rg[:, 512 * n:512 * n + 512], in0=T.r[:, 512 * n:512 * n + 512],
                             in1=GB[n % 3][:], op=AluOpType.mult).then_inc(S.ms, 2)
        else:
            for a in range(2):
                c = 512 * n + 256 * a
                ve.wait_ge(S.rs, n + 1 + a)
                ve.tensor_tensor(out=T.rg[:, c:c + 256], in0=T.r[:, c:c + 256],
                                 in1=GB[n % 3][:, 256 * a:256 * a + 256], op=AluOpType.mult).then_inc(S.ms, 1)

    if not is_rank:
        rid, pid, _se = topo.addr(workers[0])
        ve.wait_ge(YQ[0], NQ)
        ve.tensor_copy(out=T.ysb[:, 0:256], in_=YP[0][:, 0:256]).then_inc(CS[0], 1)
        se.wait_ge(YQ[1], NQ)
        se.activation(T.ysb[:, 256:512], YP[1][:, 0:256], ActivationFunctionType.Copy).then_inc(CS[1], 1)
        for a in range(2):
            c = 512 * (w - 1) + 256 * a
            g.wait_ge(CS[a], 1)
            g.remote_dma(out_ap=T.part[:, c:c + 256], in_ap=T.ysb[:, 256 * a:256 * a + 256],
                         remote_sem=S["p%d%d" % (w - 1, a)], local_sem=S.sent, pid=pid, routing_id=rid,
                         dma_engine_mask=_join(lowb if a == 0 else upb))
            nsent += 8
        g.wait_ge(S.sent, nsent)
        return

    for j, q in enumerate(qord):
        if j == 0:
            ve.wait_ge(YQ[0], NQ)
        else:
            ve.wait_ge(S.ada, j)
        ve.wait_ge(S["p%d0" % q], 8)
        c = 512 * q
        if j < NH - 1:
            ve.tensor_tensor(out=YP[0][:, 0:256], in0=YP[0][:, 0:256], in1=T.part[:, c:c + 256],
                             op=AluOpType.add).then_inc(S.ada, 1)
        else:
            ve.tensor_tensor(out=T.ysb[:, 0:256], in0=YP[0][:, 0:256], in1=T.part[:, c:c + 256],
                             op=AluOpType.add).then_inc(CS[0], 1)
    c = 512 * qord[-1] + 256
    ve.wait_ge(YQ[1], NQ + NH - 1)
    ve.wait_ge(S["p%d1" % qord[-1]], 8)
    ve.tensor_tensor(out=T.ysb[:, 256:512], in0=YP[1][:, 0:256], in1=T.part[:, c:c + 256],
                     op=AluOpType.add).then_inc(CS[1], 1)
    for a, q in enumerate((g.sync, se)):
        q.wait_ge(CS[a], 1)
        q.dma_start(T.y[:, 256 * a:256 * a + 256], T.ysb[:, 256 * a:256 * a + 256]).then_inc(S.st, 16)
    g.wait_ge(S.sent, nsent)
    g.wait_ge(S.st, 32)
